import numpy as np, ml_dtypes
CORES = [23,119,17,113]
N = 4
import mx_ref
BF = ml_dtypes.bfloat16
def cut(t, i, w=512):
    return t[:, w * i:w * i + w]
def tile(rs):
    return np.stack(rs, axis=2).reshape(128, -1).astype(BF)
def pick(q, e):
    c = np.concatenate([q[0].reshape(128, -1, 4), np.zeros((128, 1, 4), np.uint8)], axis=1); s = np.concatenate([q[1], np.ones((16, 1), np.uint8)], axis=1)
    return (np.ascontiguousarray(c[:, e].reshape(128, -1)), np.ascontiguousarray(s[:, e]))
def join(*qs):
    return (np.concatenate([q[0] for q in qs], axis=1), np.concatenate([q[1] for q in qs], axis=1))
def put(q, e, v):
    c, s = q[0].reshape(128, -1, 4).copy(), q[1].copy(); c[:, e] = v[0].reshape(128, -1, 4); s[:, e] = v[1]
    return (c.reshape(128, -1), s)
def pk(c, s):
    return (np.ascontiguousarray(c), mx_ref.live(s))
def emit(q):
    return q[0], q[1]
def f(rng, *shape):
    return mx_ref.flush((rng.standard_normal(shape, dtype=np.float32) * np.exp2(rng.integers(-2, 3, shape[:-1] + (1,)))).astype(BF))
def wide(rng, *shape, cols=0):
    v = rng.standard_normal(shape, dtype=np.float32) * np.exp2(rng.integers(-12, 13, shape)).astype(np.float32)
    if cols: v *= np.repeat(np.exp2(rng.integers(-cols, cols + 1, shape[:-2] + (1, shape[-1] // 4))) * (rng.random(shape[:-2] + (1, shape[-1] // 4)) > 0.0625), 4, axis=-1).astype(np.float32)
    return mx_ref.flush(v.astype(BF))
T, G, CS, R = 96, 128, 24, 4
def game(x, qx, w, u):
    wq = [[mx_ref.quantize(np.ascontiguousarray(cut(w[r], i))) for i in range(4)] for r in range(N)]
    uq = [mx_ref.quantize(np.ascontiguousarray(u[r])) for r in range(N)]
    wait = join(*[mx_ref.quantize(np.ascontiguousarray(qx[m])) for m in range(N)])
    s = [mx_ref.quantize(np.ascontiguousarray(x[r])) for r in range(N)]
    num = [r * T + np.arange(T) for r in range(N)]
    log, said, made, head = [[] for r in range(N)], [[] for r in range(N)], [], 0
    for t in range(R):
        for r in range(N):
            a = tile([np.maximum(mx_ref.matmul(wq[r][i], s[r]), np.float32(0)) * np.float32(0.0625) for i in range(4)])
            made.append(a)
            s[r] = mx_ref.quantize(a)
            h = mx_ref.matmul(uq[r], s[r])[:2] + np.float32(0)
            stop = np.flatnonzero(h[0] > h[1])[:CS]
            if stop.size == 0: continue
            log[r].append(pick(s[r], stop))
            said[r].extend(num[r][stop].tolist())
            g = head + np.arange(stop.size)
            s[r] = put(s[r], stop, pick(wait, G * (g % N) + g // N))
            num[r][stop] = N * T + g
            head += stop.size
    return log, said, s, num, made
def fit(d, top=2.0 ** 30):
    try:
        with np.errstate(all="ignore"):
            a = np.abs(np.stack(game(d["x"], d["qx"], d["w"], d["u"])[4]).astype(np.float32))
    except Exception: return False
    return bool(np.isfinite(a).all() and ((a == 0) | (a >= 2.0 ** -30) & (a <= top)).all())
def first(make, top=2.0 ** 30):
    for i in range(5):
        d = make()
        if fit(d, top): break
    return d
def plain(rng):
    w = np.rint(rng.standard_normal((N, 128, 2048), dtype=np.float32) * 8) * 0.125 * np.exp2(rng.integers(-1, 2, (N, 128, 1))) + 0.0
    u = np.zeros((N, 128, 512), np.float32)
    u[:, :, :8] = rng.standard_normal((N, 128, 8))
    u[:, :, 4:8] += 0.15 * rng.random((N, 1, 1))
    u *= np.exp2(rng.integers(-1, 2, (N, 128, 1)))
    return {"x": np.array(f(rng, N, 128, 4 * T)), "qx": np.array(f(rng, N, 128, 4 * G)), "w": w.astype(BF), "u": np.array(mx_ref.flush(u.astype(BF))), "v": np.array(f(rng, N, 128, 512))}
def channel(w, alone=False):
    a = w.astype(np.float32).reshape(N, 128, 4, 128, 4)
    if alone: a[:, :8] = 0
    a[:, :, :, :8, :] = 0
    for i in range(4):
        for j in range(8): a[:, j, i, j, i] = 16
    return a.reshape(N, 128, 2048).astype(BF)
def flags(d, live, wait):
    d["x"][:, :8] = np.repeat(np.where(live, 4.0, 0.0), 4, axis=1)[:, None, :].astype(BF)
    d["qx"][:, :8] = np.repeat(np.where(wait.reshape(G, N).T, 4.0, 0.0), 4, axis=1)[:, None, :].astype(BF)
def signed(t, a, b):
    o = np.abs(t.astype(np.float32))
    o[:, :4] *= a
    o[:, 4:8] *= b
    return o.astype(BF)
def setup_inputs(rng):
    return first(lambda: plain(rng), 2.0 ** 8)
def setup_inputs_many(rng):
    def make():
        d = plain(rng)
        d["w"] = channel(d["w"])
        pair = rng.integers(0, 2, N * G // 2)
        flags(d, np.stack([rng.permutation(T) < 3 * T // 4 for r in range(N)]), np.stack([pair, 1 - pair], axis=1).reshape(-1) == 1)
        for r in range(N):
            a = np.zeros((128, 512), np.float32)
            a[:8, :4] = 1
            a[8:, 4:8] = np.abs(rng.standard_normal((120, 4))) * 2.0 ** -8
            d["u"][r] = mx_ref.flush(a.astype(BF))
        return d
    return first(make)
def setup_inputs_none(rng):
    def make():
        d = plain(rng)
        a, b = rng.permutation(N)[:2]
        d["u"][a] = signed(d["u"][a], -1, 1)
        d["u"][b] = signed(d["u"][b], 1, -1)
        return d
    return first(make)
def setup_inputs_ties(rng):
    def make():
        d = plain(rng)
        d["w"] = channel(d["w"])
        flags(d, np.stack([rng.permutation(T) < T // 3 for r in range(N)]), rng.random(N * G) < 0.3)
        d["u"][:, :, 4:8] = d["u"][:, :, :4]
        d["u"][:, :8, :4] = 1
        d["u"][:, :8, 4:8] = 0
        a, c = rng.permutation(N)[:2]
        d["u"][a, :, 4:8] = d["u"][a, :, :4]
        d["u"][c] = 0
        d["u"][c, :7, :8] = 1
        d["u"][c, 7, :4] = 2.0 ** -8
        d["u"][c, 7, 4:8] = 2.0 ** -9
        return d
    return first(make)
def setup_inputs_zero(rng):
    def make():
        d = plain(rng)
        d["w"] = channel(d["w"], alone=True)
        live = np.stack([rng.permutation(np.repeat([0, 1, 2], [T - 2 * (T // 8), T // 8, T // 8])) for r in range(N)])
        for k, e in (("x", live), ("qx", rng.choice(3, (N, G), p=[0.75, 0.125, 0.125]))):
            m = np.repeat(e, 4, axis=1)[:, None, :]
            c = np.where(m == 0, d[k].astype(np.float32), np.float32(0))
            c[:, :8] = np.where(m == 2, np.float32(-4), c[:, :8])
            d[k] = c.astype(BF)
        for r in rng.permutation(N)[:N // 2]: d["u"][r] = signed(d["u"][r], 1, -1)
        return d
    return first(make)
def setup_inputs_spread(rng):
    return first(lambda: {**plain(rng), "x": wide(rng, N, 128, 4 * T, cols=6), "qx": wide(rng, N, 128, 4 * G, cols=6)})
def check_inputs(d):
    b = []
    for k in ("x", "qx", "w", "u", "v"):
        a = np.abs(d[k].astype(np.float32))
        if not (np.isfinite(a).all() and ((a == 0) | (a >= 2.0 ** -30) & (a <= 2.0 ** 30)).all()): b.append("a value of " + k)
    if (d["u"][:, :, 8:].astype(np.float32) != 0).any(): b.append("u has numbers behind its first two columns")
    if not b and not fit(d): b.append("a number that a layer makes")
    return b
def reference(x, qx, w, u, v):
    log, said, s, num, made = game(x, qx, w, u)
    M = R * CS + T
    oc, osc = np.zeros((N, 128, 4 * M), np.uint8), np.zeros((N, 16, M), np.uint8)
    sid, y = np.full((N, 1, M), -1, np.float32), np.zeros((N, 128, T), np.float32)
    for r in range(N):
        n = len(said[r])
        oc[r], osc[r] = emit(pick(join(*log[r], s[r]), np.concatenate([np.arange(n), np.full(R * CS - n, -1), n + np.arange(T)])))
        sid[r, 0, :n] = said[r]
        sid[r, 0, R * CS:] = num[r]
        y[r] = mx_ref.matmul(mx_ref.quantize(np.ascontiguousarray(v[r])), s[r])
    return {"oc": oc, "osc": osc, "sid": sid, "y": y}

@@ -1,0 +1,706 @@
+from concourse.bass import DstId, RemoteDMATransfer
+from concourse.mybir import dt, AluOpType, AxisListType, ActivationFunctionType
+
+A = AluOpType
+F = ActivationFunctionType
+f8, u8, f32, bf, i32, u16 = "float8_e4m3fn_x4", "uint8", "float32", "bfloat16", "int32", "uint16"
+L = 96
+W = 64
+SEM, FLY, ROW, MORE = 0.11, 1.35, 0.012, 1.2
+PLAN = []
+SCRATCH, CODES = {}, []
+for _w, _d, _ns in ((512, bf, "xt qt q1 vt ua ub h0"), (2048, bf, "wt"), (8, bf, "ut"), (4, bf, "nu"), (128, bf, "nul"), (1088, bf, "h1 h2 h3"),
+                    (96, f32, "y_sb"), (192, f32, "sidb"), (128, f32, "nl j16"), (144, f32, "g384"),
+                    (1, i32, "pi q16i"), (64, f32, "one lz zk"), (16, f32, "c16 pw pwr pwa pwb pwc zero q4 q5 q6 or1 ord ord6 pb pc"), (2, f32, "kb"),
+                    (32, bf, "cl1 cl2 cl3 cl4"), (112, bf, "sel cap"), (560, bf, "b1 b2 b3 b4"),
+                    (16, i32, "pwi i4"), (64, i32, "oi oj ki"), (8, u16, "lgl of"), (16, u16, "oh"), (128, f32, "f1 f2 f3 f4"),
+                    (64, u16, "o1 o2 o3 o4"), (272, f32, "num1 num2 num3 hc1 hc2 hc3"), (384, f32, "num4")):
+    for _n in _ns.split():
+        SCRATCH[_n] = ("sbuf", [128, _w], _d)
+for _w, _ns in ((128, "xq qc qf uq un vq fin lg"), (512, "wq"), (272, "sr1 sr2 sr3 cat1 cat2 cat3"), (384, "cat4"), (96, "lgo"), (256, "land1 land2 land3"), (64, "p2 p3")):
+    for _n in _ns.split():
+        SCRATCH[_n] = ("sbuf", [128, _w], f8)
+        SCRATCH[_n + "_s"] = ("sbuf", [128, _w], u8)
+        CODES.append(_n)
+for _n in ("psA", "psB", "psC", "psD"):
+    SCRATCH[_n] = ("psum", [128, 1024], f32)
+SEMAPHORES = ["ev", "es", "et", "eg", "loc", "r1", "r2", "r3", "r4"] + ["m%d%d" % (t, q) for t in range(1, 5) for q in range(4)] + ["d%d" % i for i in range(56)]
+
+
+def fan(topo, src, dsts):
+    off = [i for i, d in enumerate(dsts) if topo.chip(d) != topo.chip(src)]
+    on = [i for i, d in enumerate(dsts) if topo.chip(d) == topo.chip(src)]
+    out = [None] * len(dsts)
+    used = []
+    for part in (off, on):
+        if not part:
+            continue
+        pool = [e for e in topo.engines(src, dsts[part[0]]) if e not in used]
+        if part is on and not used:
+            pool = pool[len(pool) // 2:]
+        k = 1
+        while 2 * k * len(part) <= len(pool):
+            k *= 2
+        for j, i in enumerate(part):
+            out[i] = pool[j * k:(j + 1) * k]
+        used += pool
+    return out
+
+
+def span(v):
+    n, lo, hi = v[0], v[1], v[2]
+    if n[:2] == "ps":
+        return n, lo // 512 * 512, (hi + 511) // 512 * 512, None
+    return n, lo, hi, lo % 4 if v[3] == 4 else None
+
+
+def meet(e, lo, hi, f):
+    return e[0] < hi and e[1] > lo and (e[5] is None or f is None or e[5] == f)
+
+
+def inside(e, lo, hi, f):
+    return e[0] >= lo and e[1] <= hi and (f is None or e[5] == f)
+
+
+def program(r, T, topo):
+    C = T.cores
+    N = len(C)
+    core = C[r]
+    others = [q for q in range(N) if q != r]
+    ex = r == N - 1
+    two = r < 2
+    NR = (128, 144, 72, 96)[r]
+    NQ = max(NR, 128)
+    NP = (36, 36, 18, 24)[r]
+    n2 = 32
+    n3 = 32 if two else 48
+    nodes, seen, arrivals = [], {}, {}
+    sent, turn = [0], [0]
+
+    def rec(fns, reads, writes, late=0.0, dests=()):
+        i = len(nodes)
+        pre = set()
+        for isw, vs in ((0, reads), (1, writes)):
+            for v in vs:
+                n, lo, hi, f = span(v)
+                pre.update([e[4] for e in seen.get(n, []) if meet(e, lo, hi, f) and (e[2] or isw or n[:2] == "ps")])
+        for isw, vs in ((0, reads), (1, writes)):
+            for v in vs:
+                n, lo, hi, f = span(v)
+                h = seen.setdefault(n, [])
+                if isw:
+                    h[:] = [e for e in h if not inside(e, lo, hi, f)]
+                h.append((lo, hi, isw, "", i, f))
+        nodes.append((fns, reads, writes, min([f[2] for f in fns.values()]) if fns else 0.0, late, pre, dests))
+
+    def op(q, fn, reads, writes, cost):
+        rec({q: ("op", fn, cost)}, reads, writes)
+
+    def dma(q, out, in_, reads, writes, kib=64):
+        rec({q: ("dma", lambda e: e.dma_start(out, in_), 0.08)}, reads, writes, 1.7 + kib * 0.004)
+
+    def arrive(key, writes):
+        arrivals[key] = len(nodes)
+        rec({}, [], writes)
+
+    def V(n, lo, hi, st=1):
+        return (n, lo, hi, st)
+
+    def ap(v):
+        return T[v[0]][:, v[1]:v[2]] if v[3] == 1 else T[v[0]][:, v[1]:v[2]:v[3]]
+
+    def code(v):
+        return ap(v).bitcast(dt.uint8)
+
+    def pl(v):
+        return (v[0] + "_s",) + v[1:]
+
+    def sc(x):
+        return ap(x) if isinstance(x, tuple) else x
+
+    def rd(*xs):
+        return [x for x in xs if isinstance(x, tuple)]
+
+    def w(v):
+        return (v[2] - v[1] + v[3] - 1) // v[3]
+
+    cols = {}
+
+    def one(name):
+        i = cols.setdefault(name, len(cols))
+        return V("one", i, i + 1)
+
+    def vcost(n):
+        return 0.06 + 0.00105 * max(64, n)
+
+    def tsf(out, in0, s1, op0, s2=None, op1=None):
+        if op1 is None:
+            return lambda e: e.tensor_scalar(ap(out), ap(in0), sc(s1), None, op0)
+        return lambda e: e.tensor_scalar(ap(out), ap(in0), sc(s1), sc(s2), op0, op1)
+
+    def ts(out, in0, s1, op0, s2=None, op1=None):
+        op("v", tsf(out, in0, s1, op0, s2, op1), rd(in0, s1, s2), [out], vcost(w(out)))
+
+    def tt(out, a, b, o):
+        op("v", lambda e: e.tensor_tensor(ap(out), ap(a), ap(b), o), [a, b], [out], vcost(w(out) * (1 if a[0][:2] == "ps" else 2)))
+
+    def cp(out, a):
+        op("v", lambda e: e.tensor_copy(ap(out), ap(a)), [a], [out], vcost(w(out)))
+
+    def fill(out, c):
+        if not sent[0]:
+            return op("v", lambda e: e.memset(ap(out), c), [], [out], vcost(w(out)))
+        rec({"v": ("op", lambda e: e.memset(ap(out), c), vcost(w(out))), "g": ("op", lambda e: e.iota(ap(out), [[0, w(out)]], int(c), 0, allow_small_or_imprecise_dtypes=True), 0.14 + 0.0018 * w(out))}, [V("qc", 0, 1)], [out])
+
+    def scan(out, d0, d1, init, o0, o1):
+        op("v", lambda e: e.tensor_tensor_scan(ap(out), ap(d0), ap(d1), sc(init), o0, o1), rd(d0, d1, init), [out], vcost(w(out)))
+
+    def red(out, a):
+        op("v", lambda e: e.tensor_reduce(ap(out), ap(a), AxisListType.X, A.add), [a], [out], vcost(w(a)))
+
+    def actf(out, a, f, kw):
+        k2 = {k: sc(x) for k, x in kw.items()}
+        return lambda e: e.activation(ap(out), ap(a), f, **k2)
+
+    def act(out, a, f, **kw):
+        op("s", actf(out, a, f, kw), rd(a, kw.get("bias"), kw.get("scale")), [out] + rd(kw.get("accum_out")), vcost(w(out)) + 0.03)
+
+    def lin(out, a, mul=1.0, add=0.0, half=1.0):
+        x = 0.00105 * max(64, w(out))
+        rec({"s": ("op", actf(out, a, F.Identity, {"scale": mul, "bias": add}), x + 0.09), "v": ("op", tsf(out, a, mul, A.mult, add, A.add), 0.06 + half * x)}, rd(a, mul, add), [out])
+
+    def relu(out, a):
+        rec({"s": ("op", actf(out, a, F.Relu, {"scale": 0.0625}), vcost(w(out)) + 0.03), "v": ("op", tsf(out, a, 0.0, A.max, 0.0625, A.mult), vcost(w(out)))}, [a], [out])
+
+    def quant(out, in_):
+        op("v", lambda e: e.quantize_mx(ap(out), ap(pl(out)), ap(in_)), [in_], [out, pl(out)], 0.03 + 0.00025 * w(in_))
+
+    def mm(out, l, x, start=True, stop=True):
+        op("t", lambda e: e.matmul_mx(ap(out), ap(l), ap(pl(l)), ap(x), ap(pl(x)), start, stop), [l, pl(l), x, pl(x)], [out], 0.03 + 0.0011 * (w(x) + 16))
+
+    def pick(out, win, off):
+        op("v", lambda e: e.tensor_copy(ap(out).bitcast(dt.uint32), ap(win).bitcast(dt.uint32).indirect(ap(off))), [win, off], [out], 0.06 + 0.0014 * w(out))
+        gather(pl(out), pl(win), off)
+
+    def gather(out, win, off):
+        op("s", lambda e: e.activation(ap(out), ap(win).indirect(ap(off)), F.Copy), [win, off], [out], 0.08 + 0.0014 * w(out))
+
+    def iota(out, pattern, base, cm, isf):
+        kw = {"allow_small_or_imprecise_dtypes": True} if isf else {}
+        op("g", lambda e: e.iota(ap(out), pattern, base, cm, **kw), [], [out], 0.14 + 0.0018 * w(out))
+
+    def fused(sem, moves, size=1):
+        es = fan(topo, core, [C[m[0]] for m in moves])
+        tr, reads, dests = [], [], []
+        cost = 0.35 if sent[0] else 1.4
+        for (d, out, in_), e in zip(moves, es):
+            a = topo.addr(C[d])
+            f, n = (code, 4 * w(in_)) if in_[0] in CODES else (ap, size * w(in_))
+            tr.append(RemoteDMATransfer(dst_ids=[DstId(rid=a[0], pnc=a[1])], dma_engine_mask=sum(1 << k for k in e), remote_sem=T.sem[sem], src=f(in_), dst=f(out)))
+            reads.append(in_)
+            dests.append((d, sem, FLY + 128 * (ROW + n / 20e3) / len(e), len(e)))
+            sent[0] += len(e)
+        rec({"g": ("remote", lambda e: e.remote_dma_fused(tr, local_sem=T.sem.loc), cost)}, reads, [], 0.0, dests)
+
+    def both(sem, moves):
+        fused(sem, moves)
+        fused(sem, [(d, pl(a), pl(b)) for d, a, b in moves])
+
+    def park(out, in_):
+        dma("y", code(out), code(in_), [in_], [out])
+        dma("y", ap(pl(out)), ap(pl(in_)), [pl(in_)], [pl(out)])
+
+    def slot(m, d):
+        return W * ((m - d - 1) % N)
+
+    def land(n, b, d, lo, hi):
+        return V(n, b + slot(r, d) + lo, b + slot(r, d) + hi)
+
+    def lands(n, b, lo, hi):
+        vs = [V(n, b + W * s + lo, b + W * s + hi) for s in range(N - 1)]
+        return vs + [pl(v) for v in vs]
+    arrive("r1", lands("land1", 0, 0, 36 if two else 24))
+    if not two:
+        arrive("r2", lands("land2", 0, 0, 6))
+    arrive("r3", lands("land3", 0, 0, 6 if two else 12))
+    arrive("r4", lands("cat4", 0, 0, 6))
+    c = lambda t, q: V("cl%d" % t, 8 * q, 8 * q + 1)
+    cs = lambda t, n=4: V("cl%d" % t, 0, 8 * n - 7, 8)
+    own = lambda t: c(t, r)
+    for t in range(1, 5):
+        for q in others:
+            if t < 4 or q < N - 1:
+                arrive("m%d%d" % (t, q), [c(t, q)])
+
+    dma("y", T.ut[:], T.u[:, 0:8], [], [V("ut", 0, 8)], 4)
+    dma("s", T.q1[:, 0:144], T.qx[:, 0:144], [], [V("q1", 0, 144)], 36)
+    dma("y", T.xt[:, 0:384], T.x[:], [], [V("xt", 0, 384)], 128)
+    for i in range(4):
+        x = V("wt", 512 * i, 512 * i + 512)
+        dma("sy"[i % 2], ap(x), T.w[:, 512 * i:512 * i + 512], [], [x], 128 + 32 * i)
+    dma("s", T.qt[:], T.qx[:], [], [V("qt", 0, 512)], 400)
+    dma("y", T.vt[:], T.v[:], [], [V("vt", 0, 512)], 500)
+
+    iota(V("pi", 0, 1), [[1, 1]], 0, 1, False)
+    iota(V("c16", 0, 9), [[16, 9]], 0, 0, True)
+    iota(V("j16", 0, L), [[0, 6], [1, 16]], 0, 0, True)
+    iota(V("g384", 0, 144), [[1, 144]], 384, 0, True)
+    iota(V("num1", NQ, NQ + L), [[1, L]], L * r, 0, True)
+    q16, pw, nul = one("q16"), V("pw", 0, 9), V("nul", 0, 128)
+    fill(nul, 0.0)
+    fill(V("q1", 144, 512), 0.0)
+    fill(V("xt", 4 * L, 512), 0.0)
+    fill(V("h0", 4 * L, 512), 0.0)
+    fill(V("cap", 0, L), 24.0)
+    fill(V("b1", 0, 1), 0.0)
+    fill(V("zero", 0, 4), 0.0)
+    ts(V("q16i", 0, 1), V("pi", 0, 1), 15, A.bitwise_and)
+    cp(q16, V("q16i", 0, 1))
+    ts(pw, V("c16", 0, 9), q16, A.add)
+    cp(V("pwi", 0, 9), pw)
+    ts(V("nu", 0, 4), V("ut", 4, 8), -1.0, A.mult)
+    for i in range(4):
+        lin(V("ua", i, 512, 4), nul, 1.0, V("ut", i, i + 1), 0.5)
+        lin(V("ub", i, 512, 4), nul, 1.0, V("nu", i, i + 1), 0.5)
+
+    qc = lambda a, b: V("qc", a, b)
+    qa = lambda a, b: V("qf", a, b)
+    quant(qa(0, 128), V("q1", 0, 512))
+    both("r1", [(d, land("land1", 0, d, 0, 36), qa(0, 36)) for d in (0, 1) if d != r])
+    both("r1", [(d, land("land1", 0, d, 0, 24), qa(0, 24)) for d in (2, 3) if d != r])
+    park(V("land1", 3 * W, 3 * W + NP), qa(0, NP))
+    quant(qc(0, 128), V("qt", 0, 512))
+
+    BANKS = [("psA", 0), ("psA", 512), ("psB", 0), ("psB", 512), ("psC", 0)]
+    DB, PB, WB = ("psD", 0), ("psD", 512), ("psC", 512)
+
+    def mult(src, h, n):
+        for b in range(4):
+            p, o = BANKS[turn[0] % 5]
+            turn[0] += 1
+            mm(V(p, o, o + w(src)), V("wq", 128 * b, 128 * b + 128), src)
+            relu(V(h[0], h[1] + b, h[1] + 4 * n, 4), V(p, o, o + n))
+
+    def diff(x, bank):
+        d = V(bank[0], bank[1], bank[1] + w(x))
+        mm(d, V("uq", 0, 128), x, True, False)
+        mm(d, V("un", 0, 128), x, False, True)
+        return d
+
+    quant(V("xq", 0, 128), V("xt", 0, 512))
+    for i in range(4):
+        quant(V("wq", 128 * i, 128 * i + 128), V("wt", 512 * i, 512 * i + 512))
+    quant(V("uq", 0, 128), V("ua", 0, 512))
+    quant(V("un", 0, 128), V("ub", 0, 512))
+    s1, s2, s3, s4 = V("sr1", 0, 128), V("sr2", 0, 128), V("sr3", 0, 128), V("cat4", 256, 384)
+    mult(V("xq", 0, 128), V("h0", 0, 512), L)
+    quant(s1, V("h0", 0, 512))
+    for n, o in (("sr2", 0), ("sr3", 0), ("cat4", 256), ("fin", 0)):
+        park(V(n, o + L, o + 128), V("sr1", L, 128))
+
+    def SO(t):
+        return 256 if t == 4 else NQ if t == 1 or (t == 2 and two) else 128
+
+    def fv(t, lo, w=1):
+        return V("f%d" % t, lo, lo + w)
+    NA, M1, X1, OL, ACC = 0, 8, 16, 32, 40
+
+    def BV(t, o, lo, hi, st=1):
+        return V("b%d" % t, 112 * o + lo, 112 * o + hi, st)
+    z0 = lambda t: BV(t, 2, 15, L, 16)
+    z1 = lambda t: BV(t, 3, 15, L, 16)
+
+    def count(t, want):
+        want(BV(t, 1, 0, L))
+        scan(BV(t, 0, 1, L + 1), BV(t, 1, 0, L), V("cap", 0, L), 0.0, A.add, A.min)
+        last = BV(t, 0, L, L + 1)
+        if t < 4 or not ex:
+            fused("m%d%d" % (t, r), [(d, c(t, r), last) for d in others], 2)
+            lin(own(t), last)
+
+    def picked(t):
+        def want(out):
+            win, o = V("hc%d" % t, 0, SO(t) + 128), V("o%d" % t, 0, 6)
+            op("v", lambda e: e.tensor_scalar(ap(out), ap(win).indirect(ap(o)), 0.0, None, A.is_gt), [win, o], [out], 0.06 + 0.0014 * L)
+        return want
+
+    def fold(t):
+        scan(BV(t, 2, 0, L), V("sel", 0, L), BV(t, 0, 0, L), 0.0, A.add, A.min)
+        scan(BV(t, 3, 0, L), V("sel", 0, L), BV(t, 0, 1, L + 1), 0.0, A.add, A.min)
+        tt(fv(t, NA, 6), z0(t), z1(t), A.is_equal)
+        tt(fv(t, M1, 6), fv(t, NA, 6), pwo(t), A.mult)
+
+    def olist(t, adds=()):
+        x, i = z0(t), 0
+        while adds:
+            y = fv(t, X1 + 8 * i, 6)
+            n = 2 if adds[1:] and adds[0][0] == adds[1][0] else 1
+            ts(y, x, adds[0], A.add, *((adds[1], A.add) if n == 2 else ()))
+            x, i, adds = y, i + 1, adds[n:]
+        tt(fv(t, OL, 6), x, fv(t, M1, 6), A.max)
+        cp(V("o%d" % t, 0, 6), fv(t, OL, 6))
+
+    def signs(t):
+        for i in range(2):
+            act(BV(t, 4, 0, L), BV(t, 0, 1, L + 1), F.Sign, scale=-1.0, bias=V("kb", i, i + 1), accum_out=fv(t, ACC + i))
+
+    def logpick(t, src):
+        ts(V("o%d" % t, 8, 10), fv(t, ACC, 2), 0.5, A.mult, 48.0, A.add)
+        pick(V("lg", 32 * t - 32, 32 * t), src, V("o%d" % t, 8, 10))
+        gather(V("nl", 32 * t - 32, 32 * t), V("num%d" % t, SO(t), SO(t) + 128), V("o%d" % t, 8, 10))
+
+    def hlist(i, x, k, n=1):
+        ts(V("oh", i, i + n), x, 0.25, A.mult, k, A.add)
+        return V("oh", i, i + n)
+
+    def order(t, B, od, n):
+        ts(V("oi", 16 * t, 16 * t + n), V(od, 0, n), B, A.add, float(W), A.mult)
+        ts(V("oj", 16 * t, 16 * t + n), V("oi", 16 * t, 16 * t + n), 4 * W - 1, A.bitwise_and)
+        cp(V("o%d" % t, 16, 16 + n), V("oj", 16 * t, 16 * t + n))
+        return V("o%d" % t, 16, 16 + n)
+
+    def numbers(t, B):
+        n = min(SO(t), 144)
+        lin(V("num%d" % t, 0, n), V("g384", 0, n), 1.0, B)
+
+    def renumber(t):
+        gather(V("num%d" % (t + 1), SO(t + 1), SO(t + 1) + L), V("num%d" % t, 0, SO(t) + 128), V("o%d" % t, 0, 6))
+
+    def layer(t, src, at, n):
+        nq = w(src)
+        h, o = V("h%d" % t, 4 * at, 4 * at + 4 * nq), V("cat%d" % t, at, at + nq)
+        mult(src, h, n)
+        quant(o, h)
+        d = diff(o, PB if at else WB)
+        lin(V("hc%d" % t, at, at + nq), d)
+        if two and t == 1 and at == 0:
+            lin(V("hc2", 0, nq), d)
+
+    d1 = diff(s1, DB)
+    count(1, lambda out: ts(out, V(d1[0], d1[1], d1[1] + L), 0.0, A.is_gt))
+    ts(V("i4", 0, 9), V("pwi", 0, 9), 2, A.arith_shift_right)
+    ts(V("q4", 0, 9), V("i4", 0, 9), float(NP - 1), A.min, 1.0 / W, A.mult)
+    ts(V("pwr", 0, 9), pw, float(N - 1 - r), A.add)
+    tt(V("or1", 0, 9), V("pwr", 0, 9), V("q4", 0, 9), A.add)
+    o1 = V("o1", 16, 16 + NQ // 16)
+    order(1, 0.0, "or1", 9)
+    fill(V("h1", 4 * (NQ + L), 4 * (NQ + 128)), 0.0)
+    if NR < NQ:
+        fill(V("h1", 4 * NR, 4 * NQ), 0.0)
+    ts(V("sel", 0, L), V("j16", 0, L), q16, A.is_equal, 512.0, A.mult)
+    ts(one("qa"), q16, (3 - r) / 4 - 0.375, A.add)
+    P6 = lambda n: V(n, 0, 6)
+    ts(P6("pwa"), P6("pw"), float(NQ), A.add)
+    if two:
+        ts(P6("pwb"), P6("pw"), 128.0, A.add)
+    ts(P6("pwc"), P6("pw"), 256.0, A.add)
+
+    def pwo(t):
+        return P6("pwc") if t == 4 else P6("pwa") if SO(t) == NQ else P6("pwb")
+    pick(V("sr1", 128, 128 + NQ), V("land1", 0, 4 * W), o1)
+    layer(1, s1, NQ, L)
+    layer(1, V("sr1", 128, 128 + NQ), 0, NR)
+    fold(1)
+    olist(1, [c(1, q) for q in range(r)])
+    count(2, picked(1))
+    pick(V("sr2", 0, L), V("cat1", 0, NQ + 128), V("o1", 0, 6))
+    S1, S2, S3, K2, K3, K3a, K4, H2, H3 = [one(x) for x in "S1 S2 S3 K2 K3 K3a K4 H2 H3".split()]
+    H1 = S1
+    red(S1, cs(1))
+    lin(K2, S1, 0.25, one("qa"))
+    for t in range(2, 5):
+        fill(BV(t, 0, 0, 1), 0.0)
+    lin(V("kb", 0, 2), V("pw", 0, 2), 1.0, 0.5)
+    for t in range(1, 5):
+        fill(V("num%d" % t, SO(t) + L, SO(t) + 128), -1.0)
+    fill(V("num4", 144, 256), -1.0)
+    fill(V("pb", 0, 1), 0.0)
+    fill(V("h2", 4 * (SO(2) + L), 4 * (SO(2) + 128)), 0.0)
+    fill(V("h3", 4 * (SO(3) + L), 4 * (SO(3) + 128)), 0.0)
+    if two:
+        park(V("cat2", 0, NQ), V("cat1", 0, NQ))
+    else:
+        park(V("sr2", 128 + n2, 256), qc(0, 128 - n2))
+        fill(V("h2", 4 * n2, 512), 0.0)
+    park(V("sr3", 128 + n3, 256), qc(0, 128 - n3))
+    fill(V("h3", 4 * n3, 512), 0.0)
+    if not two:
+        ts(V("q5", 0, 3), V("i4", 0, 3), 1.0 / W, A.mult)
+        tt(V("ord", 0, 3), V("pwr", 0, 3), V("q5", 0, 3), A.add)
+    ts(V("q6", 0, 2), V("i4", 0, 2), 5.0, A.min, 1.0 / W, A.mult)
+    tt(V("ord6", 0, 2), V("pwr", 0, 2), V("q6", 0, 2), A.add)
+
+    scan(V("pc", 1, 4), cs(2, 3), V("zero", 0, 3), 0.0, A.add, A.add)
+    h = hlist(0, V("pc", 2, 4), K2, 2)
+    x, o = ("p2", 0) if two else ("land2", 3 * W - 16 if ex else 3 * W)
+    pick(V(x, o, o + 32), qc(0, 128), h)
+    both("r2", [(d, land("land2", 0, d, 0, 6), V(x, o + 16 * (d - 2), o + 16 * (d - 2) + 6)) for d in (2, 3) if d != r])
+    lin(S2, c(2, 3), 1.0, V("pc", 3, 4))
+    lin(K3, S2, 0.25, K2)
+    lin(H2, S2, 1.0, H1)
+    B2, B3, B4 = 0.0, one("B3"), one("B4")
+    fold(2)
+    if two:
+        layer(2, s2, SO(2), L)
+        olist(2, [S1, c(2, 0)][:r + 1])
+    else:
+        olist(2)
+        layer(2, s2, SO(2), L)
+        B2 = one("B2")
+        lin(B2, V("pc", r, r + 1), 1.0, H1)
+        pick(V("sr2", 128, 128 + n2), V("land2", 0, 4 * W), order(2, B2, "ord6", 2))
+        layer(2, V("sr2", 128, 256), 0, n2)
+    count(3, picked(2))
+    pick(V("sr3", 0, L), V("cat2", 0, SO(2) + 128), V("o2", 0, 6))
+    P3, oa, ob = ("p3", 32, 48) if ex else ("land3", 3 * W, 3 * W + 16) if r == 0 else ("land3", 3 * W + 16, 3 * W)
+    pick(V(P3, oa, oa + 16), qc(0, 128), hlist(4, S2, K2))
+    if r != 0:
+        both("r3", [(0, land("land3", 0, 0, 0, 6), V(P3, oa, oa + 6))])
+    pick(V(P3, ob, ob + 16), qc(0, 128), hlist(10, c(3, 0), K3))
+    if r != 2:
+        both("r3", [(2, land("land3", 0, 2, 0, 12), V(P3, ob, ob + 12))])
+    if r != 1:
+        both("r3", [(1, land("land3", 0, 1, 0, 6), V(P3, ob, ob + 6))])
+    lin(K3a, c(3, 0), 0.25, K3)
+    h = hlist(6, c(3, 1), K3a)
+    x = V("land3", 3 * W, 3 * W + 16) if ex else V("p3", 0, 16)
+    pick(x, qc(0, 128), h)
+    if not ex:
+        both("r3", [(N - 1, land("land3", 0, N - 1, 0, 12), V(x[0], x[1], x[1] + 12))])
+    layer(3, s3, SO(3), L)
+    if r == 0:
+        B3 = H2
+    elif not ex:
+        lin(B3, c(3, 0), 1.0, H2)
+    else:
+        lin(one("h20"), c(3, 0), 1.0, H2)
+        lin(B3, c(3, 1), 1.0, one("h20"))
+    gl3 = order(3, B3, "ord6", 2) if two else order(3, B3, "ord", 3)
+    pick(V("sr3", 128, 128 + n3), V("land3", 0, 4 * W), gl3)
+    layer(3, V("sr3", 128, 256), 0, n3)
+    fold(3)
+    olist(3, [] if two else [c(3, r - 1)])
+    count(4, picked(3))
+    pick(V("cat4", 256, 256 + L), V("cat3", 0, SO(3) + 128), V("o3", 0, 6))
+    red(S3, cs(3))
+    lin(K4, S3, 0.25, K3)
+    lin(H3, S3, 1.0, H2)
+    scan(V("pb", 1, 4), cs(4, 3), V("zero", 0, 3), 0.0, A.add, A.add)
+    h = hlist(12, V("pb", 0, 4), K4, 4)
+    o = 3 * W - 16 * r
+    pick(V("cat4", o, o + 64), qc(0, 128), h)
+    both("r4", [(d, land("cat4", 0, d, 0, 6), V("cat4", o + 16 * d, o + 16 * d + 6)) for d in others])
+    fold(4)
+    kq, ko, ka = [V("ki", i, i + 6) for i in (8, 16, 24)]
+    zk, zp, zm = [V("zk", i, i + 6) for i in (0, 8, 40)]
+    ts(kq, z0(4), 0.25, A.mult, -0.375, A.add)
+    ts(zk, kq, 1.0 / W, A.mult, float(N - 1 - r), A.add)
+    tt(zp, zk, z0(4), A.add)
+    if r == 0:
+        B4 = H3
+    else:
+        lin(B4, V("pb", r, r + 1), 1.0, H3)
+    ts(ko, zp, B4, A.add, float(W), A.mult)
+    ts(ka, ko, 4 * W - 1, A.bitwise_and)
+    tt(zm, ka, fv(4, M1, 6), A.max)
+    cp(V("of", 0, 6), zm)
+    for t, s, B in ((1, s1, 0.0), (2, s2, B2), (3, s3, B3)):
+        signs(t)
+        numbers(t, B)
+        logpick(t, s)
+        renumber(t)
+    lz = lambda a, w=1: V("lz", a, a + w)
+    lin(lz(1), own(1))
+    lin(lz(2), own(2), 1.0, lz(1))
+    lin(lz(3), own(3), 1.0, lz(2))
+    lin(lz(9), own(1), -1.0, 32.0)
+    lin(lz(10), own(2), -1.0, 32.0)
+    lin(lz(11), own(3), -1.0, 32.0)
+    for t in range(1, 4):
+        ts(lz(12 + 6 * t, 6), V("pw", 0, 6), lz(t), A.is_ge, lz(8 + t), A.mult)
+    tt(lz(12, 6), lz(18, 6), lz(24, 6), A.add)
+    tt(lz(36, 6), lz(30, 6), V("pw", 0, 6), A.add)
+    tt(lz(42, 6), lz(12, 6), lz(36, 6), A.add)
+    ts(V("lgl", 0, 6), lz(42, 6), 127.0, A.min)
+    signs(4)
+    logpick(4, s4)
+    pick(V("lgo", 0, 96), V("lg", 0, 128), V("lgl", 0, 6))
+    gather(V("sidb", 0, 96), V("nl", 0, 128), V("lgl", 0, 6))
+
+    def store(q, colo, src, n):
+        dma(q, T.oc[:, 4 * colo:4 * colo + 4 * n], code(src), [src], [])
+
+    def store_s(qs, colo, src, n):
+        s = pl(src)
+        for k in range(4):
+            dma(qs[k], T.osc[4 * k:4 * k + 4, colo:colo + n], T[s[0]][32 * k:32 * k + 4, s[1]:s[1] + n], [s], [])
+    store("y", 0, V("lgo", 0, 96), 96)
+    store_s("yyyy", 0, V("lgo", 0, 96), 96)
+    dma("y", T.sid[:, 0:96], T.sidb[0:1, 0:96], [V("sidb", 0, 96)], [])
+    numbers(4, B4)
+    olist(4)
+    gather(V("sidb", 96, 192), V("num4", 0, 384), V("o4", 0, 6))
+    dma("y", T.sid[:, 96:192], T.sidb[0:1, 96:192], [V("sidb", 96, 192)], [])
+    quant(V("vq", 0, 128), V("vt", 0, 512))
+    fin = V("fin", 0, 128)
+    pick(V("fin", 0, L), V("cat4", 0, 384), V("of", 0, 6))
+    mm(V("psD", 512, 640), V("vq", 0, 128), fin)
+    y, p = V("y_sb", 0, L), V("psD", 512, 512 + L)
+    store("y", 96, V("fin", 0, L), L)
+    store_s("sysy", 96, V("fin", 0, L), L)
+    rec({"v": ("op", lambda e: e.tensor_copy(ap(y), ap(p)), 0.16), "s": ("op", lambda e: e.activation(ap(y), ap(p), F.Copy), 0.19)}, [p], [y])
+    dma("s", T.y[:], T.y_sb[:], [y], [])
+    return {"nodes": nodes, "arrivals": arrivals, "sent": sent[0]}
+
+
+def joint(progs, more):
+    base, nodes = [], []
+    for p in progs:
+        base.append(len(nodes))
+        nodes += p["nodes"]
+    n = len(nodes)
+    own = [k for k, p in enumerate(progs) for _ in p["nodes"]]
+    nxt, left = [[] for _ in range(n)], [0] * n
+    for k, p in enumerate(progs):
+        for i, x in enumerate(p["nodes"]):
+            for j in x[5]:
+                y = p["nodes"][j]
+                nxt[base[k] + j].append((base[k] + i, 0.0 if "t" in x[0] and "t" in y[0] else y[4] + SEM))
+                left[base[k] + i] += 1
+            for d, key, lat, _ in x[6]:
+                j = base[d] + progs[d]["arrivals"][key]
+                nxt[base[k] + i].append((j, lat))
+                left[j] += 1
+    todo, lf, order = [i for i in range(n) if left[i] == 0], list(left), []
+    while todo:
+        i = todo.pop()
+        order.append(i)
+        for j, _ in nxt[i]:
+            lf[j] -= 1
+            if lf[j] == 0:
+                todo.append(j)
+    way = [0.0] * n
+    for i in reversed(order):
+        way[i] = nodes[i][3] + max([w + way[j] for j, w in nxt[i]] + [nodes[i][4]])
+    ready, free, avail = [0.0] * n, {}, [i for i in range(n) if left[i] == 0]
+    out = [[] for _ in progs]
+
+    def finish(i, t):
+        for j, w in nxt[i]:
+            ready[j] = max(ready[j], t + w)
+            left[j] -= 1
+            if left[j] == 0:
+                avail.append(j)
+    while avail:
+        best = None
+        for i in avail:
+            if not nodes[i][0]:
+                best = (0.0, i, None)
+                break
+            for q in nodes[i][0]:
+                s = max(free.get((own[i], q), 0.0), ready[i])
+                if best is None or s < best[0]:
+                    best = (s, i, q)
+        s, i, q = best
+        if q is None:
+            avail.remove(i)
+            finish(i, ready[i])
+            continue
+        k = own[i]
+        f = free.get((k, q), 0.0)
+        mine = [j for j in avail if own[j] == k and q in nodes[j][0]]
+        i = max([j for j in mine if max(f, ready[j]) <= s], key=lambda j: (way[j], -j))
+        end = s + nodes[i][0][q][2]
+        soon = [j for j in mine if ready[j] < end - 0.02 and way[j] > way[i] + more]
+        if soon:
+            i = max(soon, key=lambda j: (way[j], -j))
+        avail.remove(i)
+        free[(k, q)] = max(f, ready[i]) + nodes[i][0][q][2]
+        out[k].append((q, i - base[k]))
+        finish(i, free[(k, q)])
+    return out
+
+
+def rank_program(g, core, T, topo):
+    r = T.rank_of(core)
+    if r is None:
+        return
+    progs = [program(q, T, topo) for q in range(len(T.cores))]
+    if not PLAN:
+        PLAN.append(joint(progs, MORE))
+    nodes, arrivals = progs[r]["nodes"], progs[r]["arrivals"]
+    unit = {}
+    for p in progs:
+        for x in p["nodes"]:
+            for d, key, _, n in x[6]:
+                if d == r:
+                    unit[key] = unit.get(key, 0) + n
+    eng = {"v": g.vector, "s": g.scalar, "t": g.tensor, "g": g, "y": g.sync}
+    done = {"v": 0, "s": 0, "t": 0, "g": 0}
+    known = {q: {} for q in eng}
+    snap, hist, waited = {}, {}, {}
+    ndma = [0]
+
+    def deps(q, reads, writes, key):
+        need = {}
+        for isw, vs in ((0, reads), (1, writes)):
+            for v in vs:
+                n, lo, hi, f = span(v)
+                for e in hist.get(n, []):
+                    w, k, i = e[2:5]
+                    if not meet(e, lo, hi, f) or (k == key == "et" and n[:2] == "ps"):
+                        continue
+                    if not (w or isw or (n[:2] == "ps" and k != key)):
+                        continue
+                    if need.get(k, 0) < i:
+                        need[k] = i
+        for k in sorted(need):
+            i = need[k]
+            if known[q].get(k, 0) >= i:
+                continue
+            eng[q].wait_ge(T.sem[k], i * unit.get(k, 1))
+            waited[k] = max(waited.get(k, 0), i)
+            for kk, ii in snap.get((k, i), {}).items():
+                if known[q].get(kk, 0) < ii:
+                    known[q][kk] = ii
+            known[q][k] = max(known[q].get(k, 0), i)
+
+    def note(reads, writes, key, idx):
+        for isw, vs in ((0, reads), (1, writes)):
+            for v in vs:
+                n, lo, hi, f = span(v)
+                h = hist.setdefault(n, [])
+                h[:] = [e for e in h if not (inside(e, lo, hi, f) and (isw or (e[3] == key and not e[2])))]
+                h.append((lo, hi, isw, key, idx, f))
+
+    for key, i in arrivals.items():
+        note([], nodes[i][2], key, 1)
+    for q, i in PLAN[0][r]:
+        fns, reads, writes = nodes[i][:3]
+        kind, fn, _ = fns[q]
+        if kind == "op":
+            key = "e" + q
+            deps(q, reads, writes, key)
+            done[q] += 1
+            fn(eng[q]).then_inc(T.sem[key], 1)
+            snap[(key, done[q])] = dict(known[q])
+            note(reads, writes, key, done[q])
+        elif kind == "dma":
+            key = "d%d" % ndma[0]
+            ndma[0] += 1
+            unit[key] = 16
+            deps(q, reads, writes, key)
+            fn(eng[q]).then_inc(T.sem[key], 16)
+            snap[(key, 1)] = dict(known[q])
+            note(reads, writes, key, 1)
+        else:
+            deps(q, reads, [], "remote")
+            fn(eng[q])
+    for k in range(ndma[0]):
+        if waited.get("d%d" % k, 0) < 1:
+            g.sync.wait_ge(T.sem["d%d" % k], 16)
+    for q in "vstg":
+        g.wait_ge(T.sem["e" + q], done[q])
+    for k in arrivals:
+        g.wait_ge(T.sem[k], unit[k])
+    g.wait_ge(T.sem.loc, progs[r]["sent"])

@@ -6,18 +6,21 @@ F = ActivationFunctionType
 f8, u8, f32, bf, i32, u16 = "float8_e4m3fn_x4", "uint8", "float32", "bfloat16", "int32", "uint16"
 L = 96
 W = 64
-SEM, FLY, ROW, MORE = 0.11, 1.35, 0.012, 1.2
+SEM, FLY, ROW, MORE = 0.11, 1.0, 0.02, 0.6
+R1 = (((24, (3,)), (18, (2,)), (12, (1,))), ((18, (2, 0)), (24, (3,))), ((24, (3,)), (12, (1, 0))), ((18, (2,)), (12, (1, 0))))
+TRIES = 500
+CASES = ((0.0, 0.35, -0.008, 1.0, 1.0, 1.0), (-0.03, -0.2, 0.0, 0.95, 0.7, 1.1), (0.04, 0.0, 0.03, 1.1, 1.5, 0.7), (0.0, -0.3, -0.008, 1.1, 0.6, 1.0))
 PLAN = []
 SCRATCH, CODES = {}, []
-for _w, _d, _ns in ((512, bf, "xt qt q1 vt ua ub h0"), (2048, bf, "wt"), (8, bf, "ut"), (4, bf, "nu"), (128, bf, "nul"), (1088, bf, "h1 h2 h3"),
+for _w, _d, _ns in ((512, bf, "xt qt q1 vt ua ub h0"), (2048, bf, "wt"), (8, bf, "ut"), (4, bf, "nu"), (128, bf, "nul"), (768, bf, "jk"), (1088, bf, "h1 h2 h3"),
                     (96, f32, "y_sb"), (192, f32, "sidb"), (128, f32, "nl j16"), (144, f32, "g384"),
-                    (1, i32, "pi q16i"), (64, f32, "one lz zk"), (16, f32, "c16 pw pwr pwa pwb pwc zero q4 q5 q6 or1 ord ord6 pb pc"), (2, f32, "kb"),
+                    (1, i32, "pi q16i"), (64, f32, "one lz zk"), (16, f32, "c16 pw pwr pwa pwb pwc zero q4 q6 or1 ord6 pb pc t2"), (2, f32, "kb"),
                     (32, bf, "cl1 cl2 cl3 cl4"), (112, bf, "sel cap"), (560, bf, "b1 b2 b3 b4"),
-                    (16, i32, "pwi i4"), (64, i32, "oi oj ki"), (8, u16, "lgl of"), (16, u16, "oh"), (128, f32, "f1 f2 f3 f4"),
-                    (64, u16, "o1 o2 o3 o4"), (272, f32, "num1 num2 num3 hc1 hc2 hc3"), (384, f32, "num4")):
+                    (16, i32, "pwi i4"), (80, i32, "oi oj ki"), (8, u16, "lgl of"), (16, u16, "oh"), (128, f32, "f1 f2 f3 f4"),
+                    (64, u16, "o1 o2 o3 o4"), (272, f32, "num1 num2 num3 hc1 hc2 hc3"), (384, f32, "num4 yw")):
     for _n in _ns.split():
         SCRATCH[_n] = ("sbuf", [128, _w], _d)
-for _w, _ns in ((128, "xq qc qf uq un vq fin lg"), (512, "wq"), (272, "sr1 sr2 sr3 cat1 cat2 cat3"), (384, "cat4"), (96, "lgo"), (256, "land1 land2 land3"), (64, "p2 p3")):
+for _w, _ns in ((128, "xq qc qf uq un vq fin lg"), (512, "wq"), (272, "sr1 sr2 sr3 cat1 cat2 cat3"), (384, "cat4 w4"), (96, "lgo"), (256, "land1 land2 land3"), (64, "p2 p3")):
     for _n in _ns.split():
         SCRATCH[_n] = ("sbuf", [128, _w], f8)
         SCRATCH[_n + "_s"] = ("sbuf", [128, _w], u8)
@@ -68,12 +71,11 @@ def program(r, T, topo):
     core = C[r]
     others = [q for q in range(N) if q != r]
     ex = r == N - 1
-    two = r < 2
-    NR = (128, 144, 72, 96)[r]
-    NQ = max(NR, 128)
-    NP = (36, 36, 18, 24)[r]
-    n2 = 32
-    n3 = 32 if two else 48
+    NP = (12, 12, 18, 24)[r]
+    C4 = "w4" if ex else "cat4"
+
+    def SO(t):
+        return 256 if t == 4 else ((32, 32, 32), (48, 48, 48), (80, 80, 32), (96, 32, 32))[r][t - 1]
     nodes, seen, arrivals = [], {}, {}
     sent, turn = [0], [0]
 
@@ -148,9 +150,8 @@ def program(r, T, topo):
         op("v", lambda e: e.tensor_copy(ap(out), ap(a)), [a], [out], vcost(w(out)))
 
     def fill(out, c):
-        if not sent[0]:
-            return op("v", lambda e: e.memset(ap(out), c), [], [out], vcost(w(out)))
-        rec({"v": ("op", lambda e: e.memset(ap(out), c), vcost(w(out))), "g": ("op", lambda e: e.iota(ap(out), [[0, w(out)]], int(c), 0, allow_small_or_imprecise_dtypes=True), 0.14 + 0.0018 * w(out))}, [V("qc", 0, 1)], [out])
+        n = w(out) // (2 if SCRATCH[out[0]][2] == bf else 1)
+        rec({"v": ("op", lambda e: e.memset(ap(out), c), vcost(n)), "g": ("op", lambda e: e.iota(ap(out), [[0, w(out)]], int(c), 0, allow_small_or_imprecise_dtypes=True), 0.14 + 0.0018 * w(out))}, [V("qc", 0, 1)] if sent[0] else [], [out])
 
     def scan(out, d0, d1, init, o0, o1):
         op("v", lambda e: e.tensor_tensor_scan(ap(out), ap(d0), ap(d1), sc(init), o0, o1), rd(d0, d1, init), [out], vcost(w(out)))
@@ -219,21 +220,20 @@ def program(r, T, topo):
     def lands(n, b, lo, hi):
         vs = [V(n, b + W * s + lo, b + W * s + hi) for s in range(N - 1)]
         return vs + [pl(v) for v in vs]
-    arrive("r1", lands("land1", 0, 0, 36 if two else 24))
-    if not two:
-        arrive("r2", lands("land2", 0, 0, 6))
-    arrive("r3", lands("land3", 0, 0, 6 if two else 12))
-    arrive("r4", lands("cat4", 0, 0, 6))
+    arrive("r1", lands("land1", 0, 0, 24))
+    arrive("r2", lands("land2", 0, 0, 6 if ex else 18))
+    arrive("r3", lands("land3", 0, 0, 12 if r < 2 else 6))
+    arrive("r4", lands("cat4", 0, 0, 12))
     c = lambda t, q: V("cl%d" % t, 8 * q, 8 * q + 1)
     cs = lambda t, n=4: V("cl%d" % t, 0, 8 * n - 7, 8)
     own = lambda t: c(t, r)
     for t in range(1, 5):
         for q in others:
-            if t < 4 or q < N - 1:
+            if t < 4 or q < 2 or (q == 2 and ex):
                 arrive("m%d%d" % (t, q), [c(t, q)])
 
     dma("y", T.ut[:], T.u[:, 0:8], [], [V("ut", 0, 8)], 4)
-    dma("s", T.q1[:, 0:144], T.qx[:, 0:144], [], [V("q1", 0, 144)], 36)
+    dma("s", T.q1[:, 0:96], T.qx[:, 0:96], [], [V("q1", 0, 96)], 24)
     dma("y", T.xt[:, 0:384], T.x[:], [], [V("xt", 0, 384)], 128)
     for i in range(4):
         x = V("wt", 512 * i, 512 * i + 512)
@@ -245,10 +245,10 @@ def program(r, T, topo):
     iota(V("c16", 0, 9), [[16, 9]], 0, 0, True)
     iota(V("j16", 0, L), [[0, 6], [1, 16]], 0, 0, True)
     iota(V("g384", 0, 144), [[1, 144]], 384, 0, True)
-    iota(V("num1", NQ, NQ + L), [[1, L]], L * r, 0, True)
+    iota(V("num1", SO(1), SO(1) + L), [[1, L]], L * r, 0, True)
     q16, pw, nul = one("q16"), V("pw", 0, 9), V("nul", 0, 128)
     fill(nul, 0.0)
-    fill(V("q1", 144, 512), 0.0)
+    fill(V("q1", 96, 512), 0.0)
     fill(V("xt", 4 * L, 512), 0.0)
     fill(V("h0", 4 * L, 512), 0.0)
     fill(V("cap", 0, L), 24.0)
@@ -266,8 +266,8 @@ def program(r, T, topo):
     qc = lambda a, b: V("qc", a, b)
     qa = lambda a, b: V("qf", a, b)
     quant(qa(0, 128), V("q1", 0, 512))
-    both("r1", [(d, land("land1", 0, d, 0, 36), qa(0, 36)) for d in (0, 1) if d != r])
-    both("r1", [(d, land("land1", 0, d, 0, 24), qa(0, 24)) for d in (2, 3) if d != r])
+    for n, ds in R1[r]:
+        both("r1", [(d, land("land1", 0, d, 0, n), qa(0, n)) for d in ds])
     park(V("land1", 3 * W, 3 * W + NP), qa(0, NP))
     quant(qc(0, 128), V("qt", 0, 512))
 
@@ -292,14 +292,11 @@ def program(r, T, topo):
         quant(V("wq", 128 * i, 128 * i + 128), V("wt", 512 * i, 512 * i + 512))
     quant(V("uq", 0, 128), V("ua", 0, 512))
     quant(V("un", 0, 128), V("ub", 0, 512))
-    s1, s2, s3, s4 = V("sr1", 0, 128), V("sr2", 0, 128), V("sr3", 0, 128), V("cat4", 256, 384)
+    s1 = V("sr1", SO(1), SO(1) + 128)
     mult(V("xq", 0, 128), V("h0", 0, 512), L)
     quant(s1, V("h0", 0, 512))
-    for n, o in (("sr2", 0), ("sr3", 0), ("cat4", 256), ("fin", 0)):
-        park(V(n, o + L, o + 128), V("sr1", L, 128))
-
-    def SO(t):
-        return 256 if t == 4 else NQ if t == 1 or (t == 2 and two) else 128
+    for n, o in (("sr2", SO(2)), ("sr3", SO(3)), (C4, 256)) + (() if ex else (("fin", 0),)):
+        park(V(n, o + L, o + 128), V("sr1", SO(1) + L, SO(1) + 128))
 
     def fv(t, lo, w=1):
         return V("f%d" % t, lo, lo + w)
@@ -314,13 +311,15 @@ def program(r, T, topo):
         want(BV(t, 1, 0, L))
         scan(BV(t, 0, 1, L + 1), BV(t, 1, 0, L), V("cap", 0, L), 0.0, A.add, A.min)
         last = BV(t, 0, L, L + 1)
-        if t < 4 or not ex:
+        if t < 4 or r < 2:
             fused("m%d%d" % (t, r), [(d, c(t, r), last) for d in others], 2)
             lin(own(t), last)
+        elif not ex:
+            fused("m%d%d" % (t, r), [(N - 1, c(t, r), last)], 2)
 
     def picked(t):
         def want(out):
-            win, o = V("hc%d" % t, 0, SO(t) + 128), V("o%d" % t, 0, 6)
+            win, o = V("hc%d" % t, 0, SO(t) + L), V("o%d" % t, 0, 6)
             op("v", lambda e: e.tensor_scalar(ap(out), ap(win).indirect(ap(o)), 0.0, None, A.is_gt), [win, o], [out], 0.06 + 0.0014 * L)
         return want
 
@@ -342,12 +341,13 @@ def program(r, T, topo):
 
     def signs(t):
         for i in range(2):
-            act(BV(t, 4, 0, L), BV(t, 0, 1, L + 1), F.Sign, scale=-1.0, bias=V("kb", i, i + 1), accum_out=fv(t, ACC + i))
+            act(V("jk", L * (2 * t + i - 2), L * (2 * t + i - 1)), BV(t, 0, 1, L + 1), F.Sign, scale=-1.0, bias=V("kb", i, i + 1), accum_out=fv(t, ACC + i))
 
-    def logpick(t, src):
-        ts(V("o%d" % t, 8, 10), fv(t, ACC, 2), 0.5, A.mult, 48.0, A.add)
-        pick(V("lg", 32 * t - 32, 32 * t), src, V("o%d" % t, 8, 10))
-        gather(V("nl", 32 * t - 32, 32 * t), V("num%d" % t, SO(t), SO(t) + 128), V("o%d" % t, 8, 10))
+    def logpick(t):
+        a = SO(t) // 32 * 32
+        ts(V("o%d" % t, 8, 10), fv(t, ACC, 2), 0.5, A.mult, 48.0 + SO(t) - a, A.add)
+        pick(V("lg", 32 * t - 32, 32 * t), V(C4 if t == 4 else "sr%d" % t, a, SO(t) + 128), V("o%d" % t, 8, 10))
+        gather(V("nl", 32 * t - 32, 32 * t), V("num%d" % t, a, SO(t) + 128), V("o%d" % t, 8, 10))
 
     def hlist(i, x, k, n=1):
         ts(V("oh", i, i + n), x, 0.25, A.mult, k, A.add)
@@ -366,15 +366,22 @@ def program(r, T, topo):
     def renumber(t):
         gather(V("num%d" % (t + 1), SO(t + 1), SO(t + 1) + L), V("num%d" % t, 0, SO(t) + 128), V("o%d" % t, 0, 6))
 
-    def layer(t, src, at, n):
-        nq = w(src)
-        h, o = V("h%d" % t, 4 * at, 4 * at + 4 * nq), V("cat%d" % t, at, at + nq)
-        mult(src, h, n)
+    def layer(t, at, n):
+        h, o = V("h%d" % t, 4 * at, 4 * at + 512), V("cat%d" % t, at, at + 128)
+        if at:
+            fill(V(h[0], 4 * (at + L), h[2]), 0.0)
+        mult(V("sr%d" % t, at, at + 128), h, n)
         quant(o, h)
         d = diff(o, PB if at else WB)
-        lin(V("hc%d" % t, at, at + nq), d)
-        if two and t == 1 and at == 0:
-            lin(V("hc2", 0, nq), d)
+        lin(V("hc%d" % t, at, at + n), V(d[0], d[1], d[1] + n))
+
+    def layers(t, B, od):
+        layer(t, SO(t), L)
+        pick(V("sr%d" % t, 0, SO(t)), V("land%d" % t, 0, 4 * W), order(t, B, od, SO(t) // 16))
+        layer(t, 0, SO(t))
+
+    def refill(t):
+        pick(V(C4 if t == 3 else "sr%d" % (t + 1), SO(t + 1), SO(t + 1) + L), V("cat%d" % t, 0, SO(t) + L), V("o%d" % t, 0, 6))
 
     d1 = diff(s1, DB)
     count(1, lambda out: ts(out, V(d1[0], d1[1], d1[1] + L), 0.0, A.is_gt))
@@ -382,31 +389,29 @@ def program(r, T, topo):
     ts(V("q4", 0, 9), V("i4", 0, 9), float(NP - 1), A.min, 1.0 / W, A.mult)
     ts(V("pwr", 0, 9), pw, float(N - 1 - r), A.add)
     tt(V("or1", 0, 9), V("pwr", 0, 9), V("q4", 0, 9), A.add)
-    o1 = V("o1", 16, 16 + NQ // 16)
-    order(1, 0.0, "or1", 9)
-    fill(V("h1", 4 * (NQ + L), 4 * (NQ + 128)), 0.0)
-    if NR < NQ:
-        fill(V("h1", 4 * NR, 4 * NQ), 0.0)
     ts(V("sel", 0, L), V("j16", 0, L), q16, A.is_equal, 512.0, A.mult)
-    ts(one("qa"), q16, (3 - r) / 4 - 0.375, A.add)
+    lin(one("qa"), q16, 1.0, (3 - r) / 4 - 0.375)
+    lin(V("t2", 0, 2), V("pw", 0, 2), 4.0, 3 - r - 1.5)
     P6 = lambda n: V(n, 0, 6)
-    ts(P6("pwa"), P6("pw"), float(NQ), A.add)
-    if two:
-        ts(P6("pwb"), P6("pw"), 128.0, A.add)
-    ts(P6("pwc"), P6("pw"), 256.0, A.add)
+    pws = dict(zip(sorted(set([SO(t) for t in range(1, 5)])), ("pwa", "pwb", "pwc")))
+    for x in sorted(pws):
+        lin(P6(pws[x]), P6("pw"), 1.0, float(x))
 
     def pwo(t):
-        return P6("pwc") if t == 4 else P6("pwa") if SO(t) == NQ else P6("pwb")
-    pick(V("sr1", 128, 128 + NQ), V("land1", 0, 4 * W), o1)
-    layer(1, s1, NQ, L)
-    layer(1, V("sr1", 128, 128 + NQ), 0, NR)
+        return P6(pws[SO(t)])
+    layers(1, 0.0, "or1")
     fold(1)
     olist(1, [c(1, q) for q in range(r)])
     count(2, picked(1))
-    pick(V("sr2", 0, L), V("cat1", 0, NQ + 128), V("o1", 0, 6))
-    S1, S2, S3, K2, K3, K3a, K4, H2, H3 = [one(x) for x in "S1 S2 S3 K2 K3 K3a K4 H2 H3".split()]
+    refill(1)
+    S1, S2, S3, K2, K3, K3a, K4, H2, H3, P2 = [one(x) for x in "S1 S2 S3 K2 K3 K3a K4 H2 H3 P2".split()]
     H1 = S1
     red(S1, cs(1))
+    ts(V("oh", 0, 2), V("t2", 0, 2), S1, A.add, 0.25, A.mult)
+    x = V("p2", 0, 32) if ex else V("land2", 3 * W, 3 * W + 32)
+    pick(x, qc(0, 128), V("oh", 0, 2))
+    n = 12 if r == 2 else 18
+    both("r2", [(d, land("land2", 0, d, 0, n), V(x[0], x[1], x[1] + n)) for d in (2, 1, 0) if d != r])
     lin(K2, S1, 0.25, one("qa"))
     for t in range(2, 5):
         fill(BV(t, 0, 0, 1), 0.0)
@@ -415,99 +420,80 @@ def program(r, T, topo):
         fill(V("num%d" % t, SO(t) + L, SO(t) + 128), -1.0)
     fill(V("num4", 144, 256), -1.0)
     fill(V("pb", 0, 1), 0.0)
-    fill(V("h2", 4 * (SO(2) + L), 4 * (SO(2) + 128)), 0.0)
-    fill(V("h3", 4 * (SO(3) + L), 4 * (SO(3) + 128)), 0.0)
-    if two:
-        park(V("cat2", 0, NQ), V("cat1", 0, NQ))
-    else:
-        park(V("sr2", 128 + n2, 256), qc(0, 128 - n2))
-        fill(V("h2", 4 * n2, 512), 0.0)
-    park(V("sr3", 128 + n3, 256), qc(0, 128 - n3))
-    fill(V("h3", 4 * n3, 512), 0.0)
-    if not two:
-        ts(V("q5", 0, 3), V("i4", 0, 3), 1.0 / W, A.mult)
-        tt(V("ord", 0, 3), V("pwr", 0, 3), V("q5", 0, 3), A.add)
-    ts(V("q6", 0, 2), V("i4", 0, 2), 5.0, A.min, 1.0 / W, A.mult)
-    tt(V("ord6", 0, 2), V("pwr", 0, 2), V("q6", 0, 2), A.add)
+    if r >= 2:
+        ts(V("q6", 0, 2), V("i4", 0, 2), 5.0, A.min, 1.0 / W, A.mult)
+        tt(V("ord6", 0, 2), V("pwr", 0, 2), V("q6", 0, 2), A.add)
 
-    scan(V("pc", 1, 4), cs(2, 3), V("zero", 0, 3), 0.0, A.add, A.add)
-    h = hlist(0, V("pc", 2, 4), K2, 2)
-    x, o = ("p2", 0) if two else ("land2", 3 * W - 16 if ex else 3 * W)
-    pick(V(x, o, o + 32), qc(0, 128), h)
-    both("r2", [(d, land("land2", 0, d, 0, 6), V(x, o + 16 * (d - 2), o + 16 * (d - 2) + 6)) for d in (2, 3) if d != r])
-    lin(S2, c(2, 3), 1.0, V("pc", 3, 4))
+    red(P2, cs(2, 3))
+    x = V("land2", 3 * W, 3 * W + 16) if ex else V("p2", 0, 16)
+    pick(x, qc(0, 128), hlist(2, P2, K2))
+    if not ex:
+        both("r2", [(N - 1, land("land2", 0, N - 1, 0, 6), V(x[0], x[1], x[1] + 6))])
+    lin(S2, c(2, 3), 1.0, P2)
     lin(K3, S2, 0.25, K2)
     lin(H2, S2, 1.0, H1)
-    B2, B3, B4 = 0.0, one("B3"), one("B4")
+    B2, B3, B4 = H1, H2, one("B4")
     fold(2)
-    if two:
-        layer(2, s2, SO(2), L)
-        olist(2, [S1, c(2, 0)][:r + 1])
-    else:
-        olist(2)
-        layer(2, s2, SO(2), L)
+    if ex:
         B2 = one("B2")
-        lin(B2, V("pc", r, r + 1), 1.0, H1)
-        pick(V("sr2", 128, 128 + n2), V("land2", 0, 4 * W), order(2, B2, "ord6", 2))
-        layer(2, V("sr2", 128, 256), 0, n2)
+        lin(B2, P2, 1.0, H1)
+    layers(2, B2, "ord6" if ex else "or1")
+    olist(2, [] if ex else [c(2, q) for q in range(r)])
     count(3, picked(2))
-    pick(V("sr3", 0, L), V("cat2", 0, SO(2) + 128), V("o2", 0, 6))
-    P3, oa, ob = ("p3", 32, 48) if ex else ("land3", 3 * W, 3 * W + 16) if r == 0 else ("land3", 3 * W + 16, 3 * W)
-    pick(V(P3, oa, oa + 16), qc(0, 128), hlist(4, S2, K2))
-    if r != 0:
-        both("r3", [(0, land("land3", 0, 0, 0, 6), V(P3, oa, oa + 6))])
-    pick(V(P3, ob, ob + 16), qc(0, 128), hlist(10, c(3, 0), K3))
-    if r != 2:
-        both("r3", [(2, land("land3", 0, 2, 0, 12), V(P3, ob, ob + 12))])
-    if r != 1:
-        both("r3", [(1, land("land3", 0, 1, 0, 6), V(P3, ob, ob + 6))])
-    lin(K3a, c(3, 0), 0.25, K3)
-    h = hlist(6, c(3, 1), K3a)
-    x = V("land3", 3 * W, 3 * W + 16) if ex else V("p3", 0, 16)
-    pick(x, qc(0, 128), h)
-    if not ex:
-        both("r3", [(N - 1, land("land3", 0, N - 1, 0, 12), V(x[0], x[1], x[1] + 12))])
-    layer(3, s3, SO(3), L)
-    if r == 0:
-        B3 = H2
-    elif not ex:
-        lin(B3, c(3, 0), 1.0, H2)
-    else:
-        lin(one("h20"), c(3, 0), 1.0, H2)
-        lin(B3, c(3, 1), 1.0, one("h20"))
-    gl3 = order(3, B3, "ord6", 2) if two else order(3, B3, "ord", 3)
-    pick(V("sr3", 128, 128 + n3), V("land3", 0, 4 * W), gl3)
-    layer(3, V("sr3", 128, 256), 0, n3)
+    refill(2)
+    x = V("land3", 3 * W, 3 * W + 16) if r < 2 else V("p3", 32, 48)
+    pick(x, qc(0, 128), hlist(4, S2, K2))
+    both("r3", [(d, land("land3", 0, d, 0, 12), V(x[0], x[1], x[1] + 12)) for d in (1, 0) if d != r])
+    red(V("pc", 2, 3), cs(3, 2))
+    lin(K3a, V("pc", 2, 3), 0.25, K3)
+    lin(V("pc", 3, 4), c(3, 2), 1.0, V("pc", 2, 3))
+    for d, i, a, k in ((2, 6, V("pc", 2, 3), K3), (3, 8, c(3, 2), K3a)):
+        x = V("land3", 3 * W, 3 * W + 16) if r == d else V("p3", 16 * d - 32, 16 * d - 16)
+        pick(x, qc(0, 128), hlist(i, a, k))
+        if r != d:
+            both("r3", [(d, land("land3", 0, d, 0, 6), V(x[0], x[1], x[1] + 6))])
+    if r >= 2:
+        B3 = one("B3")
+        lin(B3, V("pc", r, r + 1), 1.0, H2)
+    layers(3, B3, "or1" if r < 2 else "ord6")
     fold(3)
-    olist(3, [] if two else [c(3, r - 1)])
+    olist(3, [c(3, 0)] if r == 1 else [])
     count(4, picked(3))
-    pick(V("cat4", 256, 256 + L), V("cat3", 0, SO(3) + 128), V("o3", 0, 6))
-    red(S3, cs(3))
+    refill(3)
+    lin(S3, c(3, 3), 1.0, V("pc", 3, 4))
     lin(K4, S3, 0.25, K3)
     lin(H3, S3, 1.0, H2)
-    scan(V("pb", 1, 4), cs(4, 3), V("zero", 0, 3), 0.0, A.add, A.add)
-    h = hlist(12, V("pb", 0, 4), K4, 4)
-    o = 3 * W - 16 * r
-    pick(V("cat4", o, o + 64), qc(0, 128), h)
-    both("r4", [(d, land("cat4", 0, d, 0, 6), V("cat4", o + 16 * d, o + 16 * d + 6)) for d in others])
+    scan(V("pb", 1, 3), cs(4, 2), V("zero", 0, 2), 0.0, A.add, A.add)
+    h = hlist(12, V("pb", 0, 3), K4, 3)
+    o = 3 * W - 16 * min(r, 2)
+    pick(V("cat4", o, o + 48), qc(0, 128), h)
+    far = topo.chip(C[N - 1]) != topo.chip(core)
+    n = 12 if far else 6
+    both("r4", [(d, land("cat4", 0, d, a, a + n), V("cat4", o + 16 * min(d, 2) + a, o + 16 * min(d, 2) + a + n))
+                for d, a in ((3, 0), (3, 6), (2, 0), (1, 0), (0, 0)) if d != r and not (far and a)])
     fold(4)
-    kq, ko, ka = [V("ki", i, i + 6) for i in (8, 16, 24)]
-    zk, zp, zm = [V("zk", i, i + 6) for i in (0, 8, 40)]
-    ts(kq, z0(4), 0.25, A.mult, -0.375, A.add)
-    ts(zk, kq, 1.0 / W, A.mult, float(N - 1 - r), A.add)
-    tt(zp, zk, z0(4), A.add)
     if r == 0:
         B4 = H3
     else:
-        lin(B4, V("pb", r, r + 1), 1.0, H3)
-    ts(ko, zp, B4, A.add, float(W), A.mult)
-    ts(ka, ko, 4 * W - 1, A.bitwise_and)
-    tt(zm, ka, fv(4, M1, 6), A.max)
-    cp(V("of", 0, 6), zm)
-    for t, s, B in ((1, s1, 0.0), (2, s2, B2), (3, s3, B3)):
+        lin(B4, V("pb", min(r, 2), min(r, 2) + 1), 1.0, H3)
+    if ex:
+        park(V("w4", 48, 128), qc(0, 80))
+        pick(V("w4", 0, 48), V("cat4", 0, 4 * W), order(4, B4, "or1", 3))
+        olist(4, [c(4, 2)])
+    else:
+        kq, ko, ka = [V("ki", i, i + 6) for i in (8, 16, 24)]
+        zk, zp, zm = [V("zk", i, i + 6) for i in (0, 8, 40)]
+        ts(kq, z0(4), 0.25, A.mult, -0.375, A.add)
+        ts(zk, kq, 1.0 / W, A.mult, float(N - 1 - r), A.add)
+        tt(zp, zk, z0(4), A.add)
+        ts(ko, zp, B4, A.add, float(W), A.mult)
+        ts(ka, ko, 4 * W - 1, A.bitwise_and)
+        tt(zm, ka, fv(4, M1, 6), A.max)
+        cp(V("of", 0, 6), zm)
+    for t, B in ((1, 0.0), (2, B2), (3, B3)):
         signs(t)
         numbers(t, B)
-        logpick(t, s)
+        logpick(t)
         renumber(t)
     lz = lambda a, w=1: V("lz", a, a + w)
     lin(lz(1), own(1))
@@ -523,7 +509,7 @@ def program(r, T, topo):
     tt(lz(42, 6), lz(12, 6), lz(36, 6), A.add)
     ts(V("lgl", 0, 6), lz(42, 6), 127.0, A.min)
     signs(4)
-    logpick(4, s4)
+    logpick(4)
     pick(V("lgo", 0, 96), V("lg", 0, 128), V("lgl", 0, 6))
     gather(V("sidb", 0, 96), V("nl", 0, 128), V("lgl", 0, 6))
 
@@ -538,38 +524,64 @@ def program(r, T, topo):
     store_s("yyyy", 0, V("lgo", 0, 96), 96)
     dma("y", T.sid[:, 0:96], T.sidb[0:1, 0:96], [V("sidb", 0, 96)], [])
     numbers(4, B4)
-    olist(4)
+    if not ex:
+        olist(4)
     gather(V("sidb", 96, 192), V("num4", 0, 384), V("o4", 0, 6))
     dma("y", T.sid[:, 96:192], T.sidb[0:1, 96:192], [V("sidb", 96, 192)], [])
     quant(V("vq", 0, 128), V("vt", 0, 512))
     fin = V("fin", 0, 128)
-    pick(V("fin", 0, L), V("cat4", 0, 384), V("of", 0, 6))
-    mm(V("psD", 512, 640), V("vq", 0, 128), fin)
+    pick(V("fin", 0, L), V(C4, 0, 384), V("o4" if ex else "of", 0, 6))
     y, p = V("y_sb", 0, L), V("psD", 512, 512 + L)
+    if ex:
+        mm(V("psD", 512, 640), V("vq", 0, 128), V("w4", 256, 384))
+        lin(V("yw", 256, 256 + L), p)
+        mm(V("psC", 512, 640), V("vq", 0, 128), V("w4", 0, 128))
+        lin(V("yw", 0, 48), V("psC", 512, 560))
+        fill(V("yw", 48, 256), 0.0)
+        win, o4 = V("yw", 0, 256 + L), V("o4", 0, 6)
+        rec({"v": ("op", lambda e: e.tensor_copy(ap(y), ap(win).indirect(ap(o4))), 0.2), "s": ("op", lambda e: e.activation(ap(y), ap(win).indirect(ap(o4)), F.Copy), 0.22)}, [win, o4], [y])
+    else:
+        mm(V("psD", 512, 640), V("vq", 0, 128), fin)
+        rec({"v": ("op", lambda e: e.tensor_copy(ap(y), ap(p)), 0.16), "s": ("op", lambda e: e.activation(ap(y), ap(p), F.Copy), 0.19)}, [p], [y])
     store("y", 96, V("fin", 0, L), L)
     store_s("sysy", 96, V("fin", 0, L), L)
-    rec({"v": ("op", lambda e: e.tensor_copy(ap(y), ap(p)), 0.16), "s": ("op", lambda e: e.activation(ap(y), ap(p), F.Copy), 0.19)}, [p], [y])
     dma("s", T.y[:], T.y_sb[:], [y], [])
     return {"nodes": nodes, "arrivals": arrivals, "sent": sent[0]}
 
 
 def joint(progs, more):
+    n = sum([len(p["nodes"]) for p in progs])
+    cur, x = [0.0] * n, 1
+    best = sched(progs, more, cur)
+    for _ in range(TRIES):
+        c = list(cur)
+        for _ in range(40):
+            x = (x * 1103515245 + 12345) % 2147483648
+            c[(x >> 8) % n] += (x % 251) / 250 - 0.5
+        y = sched(progs, more, c)
+        if y[0] <= best[0]:
+            best, cur = y, c
+    return best[1]
+
+
+def sched(progs, more, bias):
     base, nodes = [], []
     for p in progs:
         base.append(len(nodes))
         nodes += p["nodes"]
     n = len(nodes)
     own = [k for k, p in enumerate(progs) for _ in p["nodes"]]
-    nxt, left = [[] for _ in range(n)], [0] * n
+    nxt, left, rows, seq = [[] for _ in range(n)], [0] * n, {}, []
     for k, p in enumerate(progs):
         for i, x in enumerate(p["nodes"]):
             for j in x[5]:
                 y = p["nodes"][j]
                 nxt[base[k] + j].append((base[k] + i, 0.0 if "t" in x[0] and "t" in y[0] else y[4] + SEM))
                 left[base[k] + i] += 1
-            for d, key, lat, _ in x[6]:
+            for d, key, lat, e in x[6]:
                 j = base[d] + progs[d]["arrivals"][key]
                 nxt[base[k] + i].append((j, lat))
+                rows[(base[k] + i, j)] = max(rows.get((base[k] + i, j), 0), 128 // e)
                 left[j] += 1
     todo, lf, order = [i for i in range(n) if left[i] == 0], list(left), []
     while todo:
@@ -582,6 +594,7 @@ def joint(progs, more):
     way = [0.0] * n
     for i in reversed(order):
         way[i] = nodes[i][3] + max([w + way[j] for j, w in nxt[i]] + [nodes[i][4]])
+    way = [a + b for a, b in zip(way, bias)]
     ready, free, avail = [0.0] * n, {}, [i for i in range(n) if left[i] == 0]
     out = [[] for _ in progs]
 
@@ -604,6 +617,7 @@ def joint(progs, more):
         s, i, q = best
         if q is None:
             avail.remove(i)
+            seq.append((i, None))
             finish(i, ready[i])
             continue
         k = own[i]
@@ -617,8 +631,23 @@ def joint(progs, more):
         avail.remove(i)
         free[(k, q)] = max(f, ready[i]) + nodes[i][0][q][2]
         out[k].append((q, i - base[k]))
+        seq.append((i, q))
         finish(i, free[(k, q)])
-    return out
+    total = 0.0
+    for dsem, dfly, drow, cf, call, share in CASES:
+        rdy, fr, end = [0.0] * n, {}, 0.0
+        for i, q in seq:
+            t = rdy[i]
+            if q is not None:
+                f = nodes[i][0][q]
+                t = max(t, fr.get((own[i], q), 0.0)) + f[2] * {"op": cf, "remote": call, "dma": 1.0}[f[0]]
+                fr[(own[i], q)] = t
+            end = max(end, t + nodes[i][4])
+            for j, w in nxt[i]:
+                w += dfly + drow * rows[(i, j)] if (i, j) in rows else dsem if w else 0.0
+                rdy[j] = max(rdy[j], t + w)
+        total += share * end
+    return total, out
 
 
 def rank_program(g, core, T, topo):

@@ -1,33 +1,43 @@
+import math
 from concourse.bass import DstId, RemoteDMATransfer
-from concourse.mybir import dt, AluOpType, AxisListType, ActivationFunctionType
+from concourse.mybir import dt, AluOpType, ActivationFunctionType
 
 A = AluOpType
 F = ActivationFunctionType
 f8, u8, f32, bf, i32, u16 = "float8_e4m3fn_x4", "uint8", "float32", "bfloat16", "int32", "uint16"
 L = 96
 W = 64
-SEM, FLY, ROW, MORE = 0.11, 1.0, 0.02, 0.6
-R1 = (((24, (3,)), (18, (2,)), (12, (1,))), ((18, (2, 0)), (24, (3,))), ((24, (3,)), (12, (1, 0))), ((18, (2,)), (12, (1, 0))))
-TRIES = 500
-CASES = ((0.0, 0.35, -0.008, 1.0, 1.0, 1.0), (-0.03, -0.2, 0.0, 0.95, 0.7, 1.1), (0.04, 0.0, 0.03, 1.1, 1.5, 0.7), (0.0, -0.3, -0.008, 1.1, 0.6, 1.0))
+MODE = ["LRMM", "LLLM", "LLFM", "LMMM"]
+R1 = [("1c0+12 2c0+12", "1s0+12", "3c0+24", "3s0+24 2c12+6 2s0+24"), ("0c0+30 3c0+30", "0s0+30 3s0+30", "2c0+18", "2s0+18"),
+      ("1c0+12 0s0+48", "1s0+12", "3c0+24 0c0+24", "3s0+24 0c24+6"), ("0c0+30", "0s0+30", "2c0+18", "2s0+18 1s0+18", "1c0+12")]
+R2 = [("1c0+12 2c0+12", "1s0+24 2c12+6 2s0+24"), ("2c0+18", "2s0+18"), ("1c0+12", "1s0+12"), ("2c0+18 1c0+18", "2s0+18 1s0+18")]
+R3 = [("1c0+18", "1s0+18"), ("0c0+6", "0s0+6"), ("1c0+18 0c0+18", "1s0+18 0s0+18"), ("0c0+18 1c0+18", "0s0+18 1s0+18")]
+LOADS = "q u x 0 1 2 3 Q v"
+ONE = (0, 0, 0, 1)
+TRIES, MOVES, HEAT, EPS = 250, 14000, 0.02, 1.0
+STEP = (20, 6)
+MORE = 0.6
+CASES = [(0.11, 1.0, 0.02, 20e3, 1.0, 0.35, 1.4, 0.7, 0.015, 1.0), (0.11, 1.3, 0.012, 25e3, 0.8, 0.35, 1.2, 0.6, 0.008, 1.0),
+         (0.15, 1.2, 0.04, 15e3, 1.0, 0.5, 1.8, 1.2, 0.02, 0.3)]
 PLAN = []
 SCRATCH, CODES = {}, []
-for _w, _d, _ns in ((512, bf, "xt qt q1 vt ua ub h0"), (2048, bf, "wt"), (8, bf, "ut"), (4, bf, "nu"), (128, bf, "nul"), (768, bf, "jk"), (1088, bf, "h1 h2 h3"),
-                    (96, f32, "y_sb"), (192, f32, "sidb"), (128, f32, "nl j16"), (144, f32, "g384"),
-                    (1, i32, "pi q16i"), (64, f32, "one lz zk"), (16, f32, "c16 pw pwr pwa pwb pwc zero q4 q6 or1 ord6 pb pc t2"), (2, f32, "kb"),
-                    (32, bf, "cl1 cl2 cl3 cl4"), (112, bf, "sel cap"), (560, bf, "b1 b2 b3 b4"),
-                    (16, i32, "pwi i4"), (80, i32, "oi oj ki"), (8, u16, "lgl of"), (16, u16, "oh"), (128, f32, "f1 f2 f3 f4"),
-                    (64, u16, "o1 o2 o3 o4"), (272, f32, "num1 num2 num3 hc1 hc2 hc3"), (384, f32, "num4 yw")):
+for _w, _d, _ns in ((512, bf, "xt qt vt q1"), (2048, bf, "wt"), (768, bf, "jk"), (1024, bf, "h"),
+                    (96, f32, "y_sb"), (192, f32, "sidb"), (128, f32, "nl j16 g384 gq nul"),
+                    (16, i32, "pi qi"), (64, f32, "one lz posq"), (16, f32, "c16 pw pwq kh or1 pc pwm"), (4, f32, "kb ka"),
+                    (32, bf, "cl1 cl2 cl3 cl4"), (112, bf, "sel cap"), (1792, bf, "b"), (24, f32, "lzt lzk lzs"),
+                    (80, i32, "oi oj mi mj"), (8, u16, "lgl"), (16, u16, "oh ou"), (128, f32, "f1 f2 f3 f4"),
+                    (64, u16, "o1 o2 o3 o4"), (384, f32, "num1 num2 num3 num4 hc1 hc2 hc3")):
     for _n in _ns.split():
         SCRATCH[_n] = ("sbuf", [128, _w], _d)
-for _w, _ns in ((128, "xq qc qf uq un vq fin lg"), (512, "wq"), (272, "sr1 sr2 sr3 cat1 cat2 cat3"), (384, "cat4 w4"), (96, "lgo"), (256, "land1 land2 land3"), (64, "p2 p3")):
+for _w, _ns in ((128, "xq qc vq lg d2 d3"), (256, "uq fin"), (512, "wq land1"), (272, "sr1 sr2 sr3 sf"),
+                (384, "cat1 cat2 cat3 land2 land3 land4"), (64, "p2 p3 p4")):
     for _n in _ns.split():
         SCRATCH[_n] = ("sbuf", [128, _w], f8)
         SCRATCH[_n + "_s"] = ("sbuf", [128, _w], u8)
         CODES.append(_n)
 for _n in ("psA", "psB", "psC", "psD"):
     SCRATCH[_n] = ("psum", [128, 1024], f32)
-SEMAPHORES = ["ev", "es", "et", "eg", "loc", "r1", "r2", "r3", "r4"] + ["m%d%d" % (t, q) for t in range(1, 5) for q in range(4)] + ["d%d" % i for i in range(56)]
+SEMAPHORES = ["ev", "es", "et", "eg", "loc", "r1", "r2", "r3", "r4"] + ["m%d%d" % (t, q) for t in range(1, 5) for q in range(4)] + ["e%d" % i for i in range(40)]
 
 
 def fan(topo, src, dsts):
@@ -54,11 +64,16 @@ def span(v):
     n, lo, hi = v[0], v[1], v[2]
     if n[:2] == "ps":
         return n, lo // 512 * 512, (hi + 511) // 512 * 512, None
-    return n, lo, hi, lo % 4 if v[3] == 4 else None
+    return n, lo, hi, (v[3], lo % v[3]) if v[3] > 1 else None
 
 
 def meet(e, lo, hi, f):
-    return e[0] < hi and e[1] > lo and (e[5] is None or f is None or e[5] == f)
+    if e[0] >= hi or e[1] <= lo:
+        return False
+    for (s, a), p, q in ((e[5] or (1, 0), lo, hi), (f or (1, 0), e[0], e[1])):
+        if (a - p) % s >= q - p:
+            return False
+    return e[5] is None or f is None or (e[5][1] - f[1]) % min(e[5][0], f[0]) == 0
 
 
 def inside(e, lo, hi, f):
@@ -70,16 +85,26 @@ def program(r, T, topo):
     N = len(C)
     core = C[r]
     others = [q for q in range(N) if q != r]
+    near = [q for q in others if topo.chip(C[q]) == topo.chip(core)]
+    far = [q for q in others if q not in near]
     ex = r == N - 1
-    NP = (12, 12, 18, 24)[r]
-    C4 = "w4" if ex else "cat4"
+    mode = " " + MODE[r]
 
-    def SO(t):
-        return 256 if t == 4 else ((32, 32, 32), (48, 48, 48), (80, 80, 32), (96, 32, 32))[r][t - 1]
+    def RUN(t):
+        return ((128, 0, 32, 32), (48, 48, 80, 32), (80, 80, 32, 32), (96, 32, 32, 48))[r][t - 1]
+
+    def SW(t):
+        return ("land%d" % t, 4 * W) if mode[t] == "M" else ("sf" if mode[t] == "F" else "sr%d" % t, RUN(t))
+
+    def NO(t):
+        return 256 if mode[t] == "R" else RUN(t)
+
+    def NB(t):
+        return t - 1 if mode[t] == "R" else t
     nodes, seen, arrivals = [], {}, {}
     sent, turn = [0], [0]
 
-    def rec(fns, reads, writes, late=0.0, dests=()):
+    def rec(fns, reads, writes, io=None, dests=()):
         i = len(nodes)
         pre = set()
         for isw, vs in ((0, reads), (1, writes)):
@@ -93,13 +118,13 @@ def program(r, T, topo):
                 if isw:
                     h[:] = [e for e in h if not inside(e, lo, hi, f)]
                 h.append((lo, hi, isw, "", i, f))
-        nodes.append((fns, reads, writes, min([f[2] for f in fns.values()]) if fns else 0.0, late, pre, dests))
+        nodes.append((fns, reads, writes, min([f[2] for f in fns.values()]) if fns else 0.0, io, pre, dests))
 
     def op(q, fn, reads, writes, cost):
         rec({q: ("op", fn, cost)}, reads, writes)
 
-    def dma(q, out, in_, reads, writes, kib=64):
-        rec({q: ("dma", lambda e: e.dma_start(out, in_), 0.08)}, reads, writes, 1.7 + kib * 0.004)
+    def dma(qs, out, in_, reads, writes, rows, size):
+        rec({q: ("dma", lambda e: e.dma_start(out, in_), 0.08) for q in qs}, reads, writes, (rows, size))
 
     def arrive(key, writes):
         arrivals[key] = len(nodes)
@@ -144,31 +169,39 @@ def program(r, T, topo):
         op("v", tsf(out, in0, s1, op0, s2, op1), rd(in0, s1, s2), [out], vcost(w(out)))
 
     def tt(out, a, b, o):
-        op("v", lambda e: e.tensor_tensor(ap(out), ap(a), ap(b), o), [a, b], [out], vcost(w(out) * (1 if a[0][:2] == "ps" else 2)))
+        op("v", lambda e: e.tensor_tensor(ap(out), ap(a), ap(b), o), [a, b], [out], vcost(2 * w(out)))
 
     def cp(out, a):
         op("v", lambda e: e.tensor_copy(ap(out), ap(a)), [a], [out], vcost(w(out)))
-
-    def fill(out, c):
-        n = w(out) // (2 if SCRATCH[out[0]][2] == bf else 1)
-        rec({"v": ("op", lambda e: e.memset(ap(out), c), vcost(n)), "g": ("op", lambda e: e.iota(ap(out), [[0, w(out)]], int(c), 0, allow_small_or_imprecise_dtypes=True), 0.14 + 0.0018 * w(out))}, [V("qc", 0, 1)] if sent[0] else [], [out])
-
-    def scan(out, d0, d1, init, o0, o1):
-        op("v", lambda e: e.tensor_tensor_scan(ap(out), ap(d0), ap(d1), sc(init), o0, o1), rd(d0, d1, init), [out], vcost(w(out)))
-
-    def red(out, a):
-        op("v", lambda e: e.tensor_reduce(ap(out), ap(a), AxisListType.X, A.add), [a], [out], vcost(w(a)))
 
     def actf(out, a, f, kw):
         k2 = {k: sc(x) for k, x in kw.items()}
         return lambda e: e.activation(ap(out), ap(a), f, **k2)
 
+    def fill(out, c, qs="vg"):
+        n = w(out) // (2 if SCRATCH[out[0]][2] == bf else 1)
+        fns = {"v": ("op", lambda e: e.memset(ap(out), c), vcost(n)),
+               "g": ("op", lambda e: e.iota(ap(out), [[0, w(out)]], int(c), 0, allow_small_or_imprecise_dtypes=True), 0.14 + 0.0018 * w(out)),
+               "s": ("op", actf(out, V("nul", 0, w(out)), F.Identity, {"bias": c}), vcost(w(out)) + 0.03)}
+        rec({q: fns[q] for q in qs}, [V("nul", 0, w(out))] if "s" in qs else [], [out])
+
+    def scan(out, d0, d1, init, o0, o1):
+        two = SCRATCH[out[0]][2] == bf
+        op("v", lambda e: e.tensor_tensor_scan(ap(out), ap(d0), ap(d1), sc(init), o0, o1), rd(d0, d1, init), [out], vcost(w(out) // 2 if two else w(out)))
+
     def act(out, a, f, **kw):
         op("s", actf(out, a, f, kw), rd(a, kw.get("bias"), kw.get("scale")), [out] + rd(kw.get("accum_out")), vcost(w(out)) + 0.03)
 
-    def lin(out, a, mul=1.0, add=0.0, half=1.0):
+    def lin(out, a, mul=1.0, add=0.0):
         x = 0.00105 * max(64, w(out))
-        rec({"s": ("op", actf(out, a, F.Identity, {"scale": mul, "bias": add}), x + 0.09), "v": ("op", tsf(out, a, mul, A.mult, add, A.add), 0.06 + half * x)}, rd(a, mul, add), [out])
+        rec({"s": ("op", actf(out, a, F.Identity, {"scale": mul, "bias": add}), x + 0.09), "v": ("op", tsf(out, a, mul, A.mult, add, A.add), 0.06 + x)}, rd(a, mul, add), [out])
+
+    def plus(out, a, *xs):
+        if xs[1:] or SCRATCH[out[0]][2] == u16:
+            ts(out, a, xs[0], A.add, *((xs[1], A.add) if xs[1:] else ()))
+        else:
+            lin(out, a, 1.0, xs[0])
+        return out
 
     def relu(out, a):
         rec({"s": ("op", actf(out, a, F.Relu, {"scale": 0.0625}), vcost(w(out)) + 0.03), "v": ("op", tsf(out, a, 0.0, A.max, 0.0625, A.mult), vcost(w(out)))}, [a], [out])
@@ -183,487 +216,606 @@ def program(r, T, topo):
         op("v", lambda e: e.tensor_copy(ap(out).bitcast(dt.uint32), ap(win).bitcast(dt.uint32).indirect(ap(off))), [win, off], [out], 0.06 + 0.0014 * w(out))
         gather(pl(out), pl(win), off)
 
-    def gather(out, win, off):
-        op("s", lambda e: e.activation(ap(out), ap(win).indirect(ap(off)), F.Copy), [win, off], [out], 0.08 + 0.0014 * w(out))
+    def gather(out, win, off, mul=None):
+        if mul:
+            rec({"s": ("op", lambda e: e.activation(ap(out), ap(win).indirect(ap(off)), F.Identity, scale=mul), 0.08 + 0.0014 * w(out)),
+                 "v": ("op", lambda e: e.tensor_scalar(ap(out), ap(win).indirect(ap(off)), mul, None, A.mult), 0.06 + 0.0014 * w(out))}, [win, off], [out])
+        else:
+            rec({"s": ("op", lambda e: e.activation(ap(out), ap(win).indirect(ap(off)), F.Copy), 0.08 + 0.0014 * w(out)),
+                 "v": ("op", lambda e: e.tensor_copy(ap(out), ap(win).indirect(ap(off))), 0.06 + 0.0014 * w(out))}, [win, off], [out])
 
     def iota(out, pattern, base, cm, isf):
         kw = {"allow_small_or_imprecise_dtypes": True} if isf else {}
         op("g", lambda e: e.iota(ap(out), pattern, base, cm, **kw), [], [out], 0.14 + 0.0018 * w(out))
 
-    def fused(sem, moves, size=1):
+    def fused(moves, size=1):
         es = fan(topo, core, [C[m[0]] for m in moves])
         tr, reads, dests = [], [], []
-        cost = 0.35 if sent[0] else 1.4
-        for (d, out, in_), e in zip(moves, es):
+        for (d, out, in_, sem), e in zip(moves, es):
             a = topo.addr(C[d])
             f, n = (code, 4 * w(in_)) if in_[0] in CODES else (ap, size * w(in_))
             tr.append(RemoteDMATransfer(dst_ids=[DstId(rid=a[0], pnc=a[1])], dma_engine_mask=sum(1 << k for k in e), remote_sem=T.sem[sem], src=f(in_), dst=f(out)))
             reads.append(in_)
-            dests.append((d, sem, FLY + 128 * (ROW + n / 20e3) / len(e), len(e)))
+            dests.append((d, sem, e, n))
             sent[0] += len(e)
-        rec({"g": ("remote", lambda e: e.remote_dma_fused(tr, local_sem=T.sem.loc), cost)}, reads, [], 0.0, dests)
+        rec({"g": ("remote", lambda e: e.remote_dma_fused(tr, local_sem=T.sem.loc), 0.35)}, reads, [], None, dests)
 
-    def both(sem, moves):
-        fused(sem, moves)
-        fused(sem, [(d, pl(a), pl(b)) for d, a, b in moves])
+    def scales(moves):
+        return [(d, pl(a), pl(b), sem) for d, a, b, sem in moves]
 
-    def park(out, in_):
-        dma("y", code(out), code(in_), [in_], [out])
-        dma("y", ap(pl(out)), ap(pl(in_)), [pl(in_)], [pl(out)])
+    def both(moves):
+        fused(moves)
+        fused(scales(moves))
 
-    def slot(m, d):
-        return W * ((m - d - 1) % N)
+    def calls(t, x, cs, more=()):
+        for i, call in enumerate(cs):
+            moves = list((more, scales(more))[i]) if i < 2 else []
+            for p in call.split():
+                a, n = [int(y) for y in p[2:].split("+")]
+                f = pl if p[1] == "s" else lambda v: v
+                moves.append((int(p[0]), f(land(t, int(p[0]), a, n)), f(V(x[0], x[1] + a, x[1] + a + n)), "r%d" % t))
+            fused(moves)
 
-    def land(n, b, d, lo, hi):
-        return V(n, b + slot(r, d) + lo, b + slot(r, d) + hi)
+    def rot(t, d):
+        return [q for q in range(N) if q != d and topo.chip(C[q]) == topo.chip(C[d])][0] if t == 1 else 0 if t == 2 and d < N - 1 else d
 
-    def lands(n, b, lo, hi):
-        vs = [V(n, b + W * s + lo, b + W * s + hi) for s in range(N - 1)]
-        return vs + [pl(v) for v in vs]
-    arrive("r1", lands("land1", 0, 0, 24))
-    arrive("r2", lands("land2", 0, 0, 6 if ex else 18))
-    arrive("r3", lands("land3", 0, 0, 12 if r < 2 else 6))
-    arrive("r4", lands("cat4", 0, 0, 12))
-    c = lambda t, q: V("cl%d" % t, 8 * q, 8 * q + 1)
-    cs = lambda t, n=4: V("cl%d" % t, 0, 8 * n - 7, 8)
-    own = lambda t: c(t, r)
+    def slot(t, m, d):
+        return (2 * W if t == 1 else W) * ((m - rot(t, d) - 1) % N)
+
+    def land(t, d, lo, n):
+        return V("land%d" % t, slot(t, r, d) + lo, slot(t, r, d) + lo + n)
+
+    def BV(t, o, lo, hi, st=1):
+        return V("b", 448 * t - 448 + 112 * o + lo, 448 * t - 448 + 112 * o + hi, st)
+    for t in range(1, 5):
+        if mode[t] != "R":
+            vs = [V("sf", 0, 32)] if mode[t] == "F" else [V("land%d" % t, slot(t, q, r), slot(t, q, r) + 48) for q in others]
+            arrive("r%d" % t, vs + [pl(v) for v in vs])
+
+    def c(t, q):
+        return BV(t, 0, L, L + 1) if q == r else V("cl%d" % t, 8 * q, 8 * q + 1)
     for t in range(1, 5):
         for q in others:
             if t < 4 or q < 2 or (q == 2 and ex):
                 arrive("m%d%d" % (t, q), [c(t, q)])
 
-    dma("y", T.ut[:], T.u[:, 0:8], [], [V("ut", 0, 8)], 4)
-    dma("s", T.q1[:, 0:96], T.qx[:, 0:96], [], [V("q1", 0, 96)], 24)
-    dma("y", T.xt[:, 0:384], T.x[:], [], [V("xt", 0, 384)], 128)
+    loads = {"q": (V("q1", 0, 120), T.qx[:, 0:120]), "u": (V("xt", 120, 128), T.u[:, 0:8]), "x": (V("xt", 128, 512), T.x[:]),
+             "Q": (V("qt", 0, 512), T.qx[:]), "v": (V("vt", 0, 512), T.v[:])}
     for i in range(4):
-        x = V("wt", 512 * i, 512 * i + 512)
-        dma("sy"[i % 2], ap(x), T.w[:, 512 * i:512 * i + 512], [], [x], 128 + 32 * i)
-    dma("s", T.qt[:], T.qx[:], [], [V("qt", 0, 512)], 400)
-    dma("y", T.vt[:], T.v[:], [], [V("vt", 0, 512)], 500)
+        loads[str(i)] = (V("wt", 512 * i, 512 * i + 512), T.w[:, 512 * i:512 * i + 512])
+    for i, k in enumerate(LOADS.split()):
+        dma("sy"[i % 2], ap(loads[k][0]), loads[k][1], [], [loads[k][0]], 8, 2 * w(loads[k][0]))
+    lin(V("xt", 124, 128), V("xt", 124, 128), -1.0)
 
-    iota(V("pi", 0, 1), [[1, 1]], 0, 1, False)
-    iota(V("c16", 0, 9), [[16, 9]], 0, 0, True)
+    iota(V("pi", 0, 16), [[0, 16]], 0, 1, False)
+    iota(V("c16", 0, 16), [[16, 16]], 0, 0, True)
     iota(V("j16", 0, L), [[0, 6], [1, 16]], 0, 0, True)
-    iota(V("g384", 0, 144), [[1, 144]], 384, 0, True)
-    iota(V("num1", SO(1), SO(1) + L), [[1, L]], L * r, 0, True)
-    q16, pw, nul = one("q16"), V("pw", 0, 9), V("nul", 0, 128)
-    fill(nul, 0.0)
-    fill(V("q1", 96, 512), 0.0)
-    fill(V("xt", 4 * L, 512), 0.0)
-    fill(V("h0", 4 * L, 512), 0.0)
-    fill(V("cap", 0, L), 24.0)
-    fill(V("b1", 0, 1), 0.0)
-    fill(V("zero", 0, 4), 0.0)
-    ts(V("q16i", 0, 1), V("pi", 0, 1), 15, A.bitwise_and)
-    cp(q16, V("q16i", 0, 1))
-    ts(pw, V("c16", 0, 9), q16, A.add)
-    cp(V("pwi", 0, 9), pw)
-    ts(V("nu", 0, 4), V("ut", 4, 8), -1.0, A.mult)
-    for i in range(4):
-        lin(V("ua", i, 512, 4), nul, 1.0, V("ut", i, i + 1), 0.5)
-        lin(V("ub", i, 512, 4), nul, 1.0, V("nu", i, i + 1), 0.5)
+    iota(V("g384", 0, 128), [[1, 128]], 384, 0, True)
+    q16, pw, pwq = V("pw", 0, 1), V("pw", 0, 9), V("pwq", 0, 9)
+    HS = 4 * max([RUN(t) for t in (1, 2, 3)])
+    hs = V("h", HS, HS + 512)
+    fill(V("h", HS + 4 * L, HS + 512), 0.0)
+    if not r:
+        fill(V("h", HS - 32, HS), 0.0)
+    fill(V("nul", 0, 32), 0.0)
+    fill(V("cap", 0, L), 6.0)
+    fill(V("b", 0, 1792, 448), 0.0)
+    fill(V("posq", 0, 64), 0.0)
+    ts(V("ou", 0, 16), V("c16", 0, 16), 128.0, A.is_ge, 30.0, A.add)
+    ts(V("qi", 0, 9), V("pi", 0, 9), 15, A.bitwise_and)
+    tt(pw, V("qi", 0, 9), V("c16", 0, 9), A.add)
+    lin(pwq, pw, 0.25)
 
-    qc = lambda a, b: V("qc", a, b)
-    qa = lambda a, b: V("qf", a, b)
-    quant(qa(0, 128), V("q1", 0, 512))
-    for n, ds in R1[r]:
-        both("r1", [(d, land("land1", 0, d, 0, n), qa(0, n)) for d in ds])
-    park(V("land1", 3 * W, 3 * W + NP), qa(0, NP))
-    quant(qc(0, 128), V("qt", 0, 512))
+    qc, xq = V("qc", 0, 128), V("xq", 0, 128)
+    fill(V("q1", 120, 512), 0.0)
+    fill(V("xt", 0, 120), 0.0)
+    quant(land(1, r, 0, 128), V("q1", 0, 512))
+    quant(xq, V("xt", 0, 512))
+    calls(1, land(1, r, 0, 128), R1[r])
+    for i in range(4):
+        quant(V("wq", 128 * i, 128 * i + 128), V("wt", 512 * i, 512 * i + 512))
+    for i in range(2):
+        pick(V("uq", 128 * i, 128 * i + 128), V("xq", 0, 32), V("ou", 8 * i, 8 * i + 8))
+    quant(qc, V("qt", 0, 512))
+    for t in (1, 2, 3):
+        if mode[t] in "LR":
+            fill(V("o%d" % t, 6, 8), NO(t) + L, "v")
+        else:
+            quant(V("d%d" % t, 0, 128), V("xt", 0, 512))
+    quant(V("fin", L, L + 128), V("xt", 0, 512))
 
     BANKS = [("psA", 0), ("psA", 512), ("psB", 0), ("psB", 512), ("psC", 0)]
     DB, PB, WB = ("psD", 0), ("psD", 512), ("psC", 512)
 
-    def mult(src, h, n):
+    def mult(src, h, n, at=0):
         for b in range(4):
             p, o = BANKS[turn[0] % 5]
             turn[0] += 1
             mm(V(p, o, o + w(src)), V("wq", 128 * b, 128 * b + 128), src)
-            relu(V(h[0], h[1] + b, h[1] + 4 * n, 4), V(p, o, o + n))
+            relu(V(h[0], h[1] + b, h[1] + 4 * n, 4), V(p, o + at, o + at + n))
 
     def diff(x, bank):
         d = V(bank[0], bank[1], bank[1] + w(x))
         mm(d, V("uq", 0, 128), x, True, False)
-        mm(d, V("un", 0, 128), x, False, True)
+        mm(d, V("uq", 128, 256), x, False, True)
         return d
-
-    quant(V("xq", 0, 128), V("xt", 0, 512))
-    for i in range(4):
-        quant(V("wq", 128 * i, 128 * i + 128), V("wt", 512 * i, 512 * i + 512))
-    quant(V("uq", 0, 128), V("ua", 0, 512))
-    quant(V("un", 0, 128), V("ub", 0, 512))
-    s1 = V("sr1", SO(1), SO(1) + 128)
-    mult(V("xq", 0, 128), V("h0", 0, 512), L)
-    quant(s1, V("h0", 0, 512))
-    for n, o in (("sr2", SO(2)), ("sr3", SO(3)), (C4, 256)) + (() if ex else (("fin", 0),)):
-        park(V(n, o + L, o + 128), V("sr1", SO(1) + L, SO(1) + 128))
-
-    def fv(t, lo, w=1):
-        return V("f%d" % t, lo, lo + w)
-    NA, M1, X1, OL, ACC = 0, 8, 16, 32, 40
-
-    def BV(t, o, lo, hi, st=1):
-        return V("b%d" % t, 112 * o + lo, 112 * o + hi, st)
-    z0 = lambda t: BV(t, 2, 15, L, 16)
-    z1 = lambda t: BV(t, 3, 15, L, 16)
 
     def count(t, want):
         want(BV(t, 1, 0, L))
         scan(BV(t, 0, 1, L + 1), BV(t, 1, 0, L), V("cap", 0, L), 0.0, A.add, A.min)
-        last = BV(t, 0, L, L + 1)
-        if t < 4 or r < 2:
-            fused("m%d%d" % (t, r), [(d, c(t, r), last) for d in others], 2)
-            lin(own(t), last)
-        elif not ex:
-            fused("m%d%d" % (t, r), [(N - 1, c(t, r), last)], 2)
+        if t < 4 or not ex:
+            fused([(d, V("cl%d" % t, 8 * r, 8 * r + 1), c(t, r), "m%d%d" % (t, r)) for d in (others if t < 4 or r < 2 else [N - 1])], 2)
 
-    def picked(t):
-        def want(out):
-            win, o = V("hc%d" % t, 0, SO(t) + L), V("o%d" % t, 0, 6)
-            op("v", lambda e: e.tensor_scalar(ap(out), ap(win).indirect(ap(o)), 0.0, None, A.is_gt), [win, o], [out], 0.06 + 0.0014 * L)
-        return want
+    def straight(t, src, at=0):
+        n, o = SW(t)
+        s = V(n, o, o + 128)
+        mult(src, hs, L, at)
+        quant(s, hs)
+        d = diff(s, DB)
+        count(t, lambda out: ts(out, V(d[0], d[1], d[1] + L), 0.0, A.is_gt, 0.25, A.mult))
+
+    straight(1, xq, 32)
+
+    K0 = V("kh", 0, 1)
+    lin(V("kh", 0, 2), V("pw", 0, 2), 1.0, (3 - r) / 4 - 0.375)
+    ts(V("sel", 0, L), V("j16", 0, L), q16, A.is_equal, 512.0, A.mult)
+    nq, ec, kn = one("nq"), one("ec"), one("kn")
+    ts(V("pc", 0, 8), V("pw", 0, 8), (119.0, 71.0, 71.0, 95.0)[r], A.min)
+    if r in (1, 2):
+        lin(nq, q16, -1.0, 0.375 - 0.375 / (4 * W))
+        lin(V("or1", 0, 5), V("pc", 0, 5), (W + 0.25) / (4 * W), nq)
+        lin(V("or1", 8, 13), V("or1", 0, 5), 1.0, r / 4)
+    lin(kn, K0, -1.0)
+    lin(ec, q16, -4.0 * W, 1.5 * W - 0.375)
+    lin(V("pwm", 0, 6), V("pw", 0, 6), 1.0, 4.0 * W)
+    lin(V("gq", 0, 128), V("g384", 0, 128), 0.25, kn)
+    lin(V("num1", NO(1), NO(1) + L), V("g384", 0, L), 0.25, (L * r - 384) / 4)
+    lin(V("kb", 0, 2), V("pwq", 0, 2), 1.0, 0.125)
+    pos = {}
+    for t in range(1, 5):
+        if NO(t) not in pos:
+            a = 12 * len(pos)
+            pos[NO(t)] = V("posq", a, a + 12)
+            lin(V("posq", a + 1, a + 12, 2), V("pwq", 0, 6), 1.0, NO(t) / 4)
+        fill(V("num%d" % NB(t), NO(t) + L, NO(t) + L + (32 if mode[t:t + 2] == "LR" else 8)), -0.25, "vs")
+
+    def fv(t, lo, hi, st=1):
+        return V("f%d" % t, lo, hi, st)
+    z0 = lambda t: BV(t, 2, 15, L, 16)
+    z1 = lambda t: BV(t, 3, 15, L, 16)
+    na = lambda t: BV(t, 2, 7, L, 16)
+    O = lambda t: V("o%d" % t, 0, 6)
+    adds = lambda t: [c(t, q) for q in sorted(range(r), key=lambda q: q in far)][(0, 0, N if ex else 0, 0 if r < 2 else N, 0)[t]:] if t < 4 else [c(4, 2)] if ex else []
 
     def fold(t):
         scan(BV(t, 2, 0, L), V("sel", 0, L), BV(t, 0, 0, L), 0.0, A.add, A.min)
         scan(BV(t, 3, 0, L), V("sel", 0, L), BV(t, 0, 1, L + 1), 0.0, A.add, A.min)
-        tt(fv(t, NA, 6), z0(t), z1(t), A.is_equal)
-        tt(fv(t, M1, 6), fv(t, NA, 6), pwo(t), A.mult)
+        tt(na(t), z0(t), z1(t), A.is_equal)
 
-    def olist(t, adds=()):
-        x, i = z0(t), 0
-        while adds:
-            y = fv(t, X1 + 8 * i, 6)
-            n = 2 if adds[1:] and adds[0][0] == adds[1][0] else 1
-            ts(y, x, adds[0], A.add, *((adds[1], A.add) if n == 2 else ()))
-            x, i, adds = y, i + 1, adds[n:]
-        tt(fv(t, OL, 6), x, fv(t, M1, 6), A.max)
-        cp(V("o%d" % t, 0, 6), fv(t, OL, 6))
+    def olist(t):
+        xs = adds(t)
+        if mode[t] == "R":
+            xs = [one("H")]
+            lin(xs[0], K4, 1.0, kn)
+        while xs:
+            n = 2 - len(xs) % 2
+            plus(z0(t), z0(t), *xs[:n])
+            xs = xs[n:]
+        scan(fv(t, 0, 12), pos[NO(t)], BV(t, 2, 7, L, 8), 0.0, A.mult, A.max)
+        ts(O(t), fv(t, 1, 12, 2), 4.0, A.mult)
 
-    def signs(t):
-        for i in range(2):
-            act(V("jk", L * (2 * t + i - 2), L * (2 * t + i - 1)), BV(t, 0, 1, L + 1), F.Sign, scale=-1.0, bias=V("kb", i, i + 1), accum_out=fv(t, ACC + i))
+    def mlist(t, K):
+        e = one("e%d" % t)
+        lin(e, K, 4.0 * W, ec)
+        for i, x in enumerate(adds(t)):
+            e, y = one("e%d%d" % (t, i)), e
+            lin(e, x, 4.0 * W + 1, y)
+        tt(fv(t, 16, 22), na(t), V("pwm", 0, 6), A.mult)
+        a, b = V("mi", 16 * t, 16 * t + 6), V("mj", 16 * t, 16 * t + 6)
+        ts(a, z0(t), 4.0 * W + 1, A.mult, e, A.add)
+        ts(b, a, 4 * W - 1, A.bitwise_and)
+        tt(fv(t, 24, 30), b, fv(t, 16, 22), A.max)
+        cp(V("o%d" % t, 32, 38), fv(t, 24, 30))
+        return V("o%d" % t, 32, 38)
 
-    def logpick(t):
-        a = SO(t) // 32 * 32
-        ts(V("o%d" % t, 8, 10), fv(t, ACC, 2), 0.5, A.mult, 48.0 + SO(t) - a, A.add)
-        pick(V("lg", 32 * t - 32, 32 * t), V(C4 if t == 4 else "sr%d" % t, a, SO(t) + 128), V("o%d" % t, 8, 10))
-        gather(V("nl", 32 * t - 32, 32 * t), V("num%d" % t, a, SO(t) + 128), V("o%d" % t, 8, 10))
-
-    def hlist(i, x, k, n=1):
-        ts(V("oh", i, i + n), x, 0.25, A.mult, k, A.add)
-        return V("oh", i, i + n)
-
-    def order(t, B, od, n):
-        ts(V("oi", 16 * t, 16 * t + n), V(od, 0, n), B, A.add, float(W), A.mult)
-        ts(V("oj", 16 * t, 16 * t + n), V("oi", 16 * t, 16 * t + n), 4 * W - 1, A.bitwise_and)
+    def order(t, K):
+        n = RUN(t) // 16
+        a, x = (8 if rot(t, r) != r else 0), (2 * W if t == 1 else W)
+        if t == 1:
+            ts(V("oi", 16, 16 + n), V("pc", 0, n), x + 0.25, A.mult, x * (3 - rot(t, r)) - 0.375, A.add)
+        else:
+            ts(V("oi", 16 * t, 16 * t + n), V("or1", a, a + n), K, A.add, 4.0 * W, A.mult)
+        ts(V("oj", 16 * t, 16 * t + n), V("oi", 16 * t, 16 * t + n), 4 * x - 1, A.bitwise_and)
         cp(V("o%d" % t, 16, 16 + n), V("oj", 16 * t, 16 * t + n))
-        return V("o%d" % t, 16, 16 + n)
+        pick(V(SW(t)[0], 0, RUN(t)), V("land%d" % t, 0, 3 * x + ((30, 12, 18, 24)[r] if t < 3 else W)), V("o%d" % t, 16, 16 + n))
 
-    def numbers(t, B):
-        n = min(SO(t), 144)
-        lin(V("num%d" % t, 0, n), V("g384", 0, n), 1.0, B)
-
-    def renumber(t):
-        gather(V("num%d" % (t + 1), SO(t + 1), SO(t + 1) + L), V("num%d" % t, 0, SO(t) + 128), V("o%d" % t, 0, 6))
-
-    def layer(t, at, n):
-        h, o = V("h%d" % t, 4 * at, 4 * at + 512), V("cat%d" % t, at, at + 128)
-        if at:
-            fill(V(h[0], 4 * (at + L), h[2]), 0.0)
+    def layer(t, at, n, wide):
+        a = HS - 4 * (RUN(t) - at)
+        to = NO(t) if mode[t] == "R" else at
+        h, o = V("h", a, a + 512), V("cat%d" % NB(t), to, to + 128)
         mult(V("sr%d" % t, at, at + 128), h, n)
         quant(o, h)
-        d = diff(o, PB if at else WB)
-        lin(V("hc%d" % t, at, at + n), V(d[0], d[1], d[1] + n))
+        d = diff(o, PB if to else WB)
+        lin(V("hc%d" % NB(t), to, to + wide), V(d[0], d[1], d[1] + wide))
 
-    def layers(t, B, od):
-        layer(t, SO(t), L)
-        pick(V("sr%d" % t, 0, SO(t)), V("land%d" % t, 0, 4 * W), order(t, B, od, SO(t) // 16))
-        layer(t, 0, SO(t))
+    def log(t, K):
+        for i in range(2):
+            act(V("jk", L * (2 * t + i - 2), L * (2 * t + i - 1)), BV(t, 0, 1, L + 1), F.Sign, scale=-1.0, bias=V("kb", i, i + 1), accum_out=fv(t, 40 + i, 41 + i))
+        n, o = SW(t)
+        a = o // 32 * 32
+        ls = V("o%d" % t, 8, 10)
+        ts(ls, fv(t, 40, 42), 0.5, A.mult, 48.0 + o - a, A.add)
+        pick(V("lg", 32 * t - 32, 32 * t), V(n, a, o + 128), ls)
+        num = "num%d" % NB(t)
+        if mode[t] != "R":
+            lin(V(num, 0, NO(t)), V("gq", 0, NO(t)), 1.0, K)
+        gather(V("nl", 32 * t - 32, 32 * t), V(num, NO(t) - o + a, NO(t) + L + 8), ls)
+        if t < 4:
+            gather(V("num%d" % NB(t + 1), NO(t + 1), NO(t + 1) + L), V(num, 0, NO(t) + L + 8), O(t))
 
-    def refill(t):
-        pick(V(C4 if t == 3 else "sr%d" % (t + 1), SO(t + 1), SO(t + 1) + L), V("cat%d" % t, 0, SO(t) + L), V("o%d" % t, 0, 6))
+    def step(t, K):
+        n, o = SW(t)
+        fold(t)
+        if mode[t] in "LR":
+            layer(t, o, L, 128 if mode[t:t + 2] == "LR" else L)
+            if mode[t] == "L":
+                order(t, K)
+                if (r, t) == (1, 3):
+                    ts(V("ka", 2, 4), V("pwq", 0, 2), 5.75, A.min, c(3, 0), A.add)
+                    ts(V("oh", 12, 14), V("ka", 2, 4), c(3, 1), A.add, 4.0, A.mult)
+                    pick(V("p4", 0, 32), V("sr3", 0, o), V("oh", 12, 14))
+                    both([(2, V("sf", 0, 24), V("p4", 0, 24), "r3")])
+                layer(t, 0, min(o, (120, 48, 80, 96)[r]), o)
+            olist(t)
+            o = NO(t)
+            win = V("hc%d" % NB(t), 0, o + L)
+            count(t + 1, lambda out: op("v", lambda e: e.tensor_scalar(ap(out), ap(win).indirect(ap(O(t))), 0.0, 0.25, A.is_gt, A.mult), [win, O(t)], [out], 0.06 + 0.0014 * L))
+            m, a = SW(t + 1)
+            pick(V(m, a, a + 128), V("cat%d" % NB(t), 0, o + 128), V("o%d" % t, 0, 8))
+        else:
+            if mode[t] == "F":
+                olist(t)
+            pick(V("d%d" % t, 0, L), V(n, 0, o + L), O(t) if mode[t] == "F" else mlist(t, K))
+            straight(t + 1, V("d%d" % t, 0, 128))
+            if mode[t] == "M":
+                olist(t)
+        log(t, K)
 
-    d1 = diff(s1, DB)
-    count(1, lambda out: ts(out, V(d1[0], d1[1], d1[1] + L), 0.0, A.is_gt))
-    ts(V("i4", 0, 9), V("pwi", 0, 9), 2, A.arith_shift_right)
-    ts(V("q4", 0, 9), V("i4", 0, 9), float(NP - 1), A.min, 1.0 / W, A.mult)
-    ts(V("pwr", 0, 9), pw, float(N - 1 - r), A.add)
-    tt(V("or1", 0, 9), V("pwr", 0, 9), V("q4", 0, 9), A.add)
-    ts(V("sel", 0, L), V("j16", 0, L), q16, A.is_equal, 512.0, A.mult)
-    lin(one("qa"), q16, 1.0, (3 - r) / 4 - 0.375)
-    lin(V("t2", 0, 2), V("pw", 0, 2), 4.0, 3 - r - 1.5)
-    P6 = lambda n: V(n, 0, 6)
-    pws = dict(zip(sorted(set([SO(t) for t in range(1, 5)])), ("pwa", "pwb", "pwc")))
-    for x in sorted(pws):
-        lin(P6(pws[x]), P6("pw"), 1.0, float(x))
+    def stage(t, at, ls, mine=None):
+        x = V("p%d" % t, at, at + 16 * w(ls)) if mine is None else land(t, r, -mine, 16 * w(ls))
+        pick(x, qc, ls)
+        return x
 
-    def pwo(t):
-        return P6(pws[SO(t)])
-    layers(1, 0.0, "or1")
-    fold(1)
-    olist(1, [c(1, q) for q in range(r)])
-    count(2, picked(1))
-    refill(1)
-    S1, S2, S3, K2, K3, K3a, K4, H2, H3, P2 = [one(x) for x in "S1 S2 S3 K2 K3 K3a K4 H2 H3 P2".split()]
-    H1 = S1
-    red(S1, cs(1))
-    ts(V("oh", 0, 2), V("t2", 0, 2), S1, A.add, 0.25, A.mult)
-    x = V("p2", 0, 32) if ex else V("land2", 3 * W, 3 * W + 32)
-    pick(x, qc(0, 128), V("oh", 0, 2))
-    n = 12 if r == 2 else 18
-    both("r2", [(d, land("land2", 0, d, 0, n), V(x[0], x[1], x[1] + n)) for d in (2, 1, 0) if d != r])
-    lin(K2, S1, 0.25, one("qa"))
-    for t in range(2, 5):
-        fill(BV(t, 0, 0, 1), 0.0)
-    lin(V("kb", 0, 2), V("pw", 0, 2), 1.0, 0.5)
-    for t in range(1, 5):
-        fill(V("num%d" % t, SO(t) + L, SO(t) + 128), -1.0)
-    fill(V("num4", 144, 256), -1.0)
-    fill(V("pb", 0, 1), 0.0)
-    if r >= 2:
-        ts(V("q6", 0, 2), V("i4", 0, 2), 5.0, A.min, 1.0 / W, A.mult)
-        tt(V("ord6", 0, 2), V("pwr", 0, 2), V("q6", 0, 2), A.add)
+    def part(t, x, d, a, n, lo=0):
+        return (d, land(t, d, lo, n), V(x[0], x[1] + a, x[1] + a + n), "r%d" % t)
+    oh = lambda i, n=1: V("oh", i, i + n)
+    K4, K7, Kb, K8, K9, K10, K12, K13 = [one("K%d" % i) for i in range(8)]
 
-    red(P2, cs(2, 3))
-    x = V("land2", 3 * W, 3 * W + 16) if ex else V("p2", 0, 16)
-    pick(x, qc(0, 128), hlist(2, P2, K2))
-    if not ex:
-        both("r2", [(N - 1, land("land2", 0, N - 1, 0, 6), V(x[0], x[1], x[1] + 6))])
-    lin(S2, c(2, 3), 1.0, P2)
-    lin(K3, S2, 0.25, K2)
-    lin(H2, S2, 1.0, H1)
-    B2, B3, B4 = H1, H2, one("B4")
-    fold(2)
+    step(1, K0)
+    ka = plus(V("ka", 0, 2), V("kh", 0, 2), c(1, r), c(1, near[0]))
+    calls(2, stage(2, 0, plus(oh(0, 2), ka, c(1, far[0]), c(1, far[1])), 0 if r in (1, 2) else None), R2[r])
+    plus(K4, V("ka", 0, 1), c(1, far[0]), c(1, far[1]))
+    x = [q for q in [r] + near if q < N - 1]
+    plus(Kb, K4, *[c(2, q) for q in x])
+    a = part(2, stage(2, 32, plus(oh(2), Kb, *[c(2, q) for q in far if q < N - 1]), 0 if ex else None), 3, 0, 6)
+    join = N - 1 in near
+    if not ex and not join:
+        both([a])
     if ex:
-        B2 = one("B2")
-        lin(B2, P2, 1.0, H1)
-    layers(2, B2, "ord6" if ex else "or1")
-    olist(2, [] if ex else [c(2, q) for q in range(r)])
-    count(3, picked(2))
-    refill(2)
-    x = V("land3", 3 * W, 3 * W + 16) if r < 2 else V("p3", 32, 48)
-    pick(x, qc(0, 128), hlist(4, S2, K2))
-    both("r3", [(d, land("land3", 0, d, 0, 12), V(x[0], x[1], x[1] + 12)) for d in (1, 0) if d != r])
-    red(V("pc", 2, 3), cs(3, 2))
-    lin(K3a, V("pc", 2, 3), 0.25, K3)
-    lin(V("pc", 3, 4), c(3, 2), 1.0, V("pc", 2, 3))
-    for d, i, a, k in ((2, 6, V("pc", 2, 3), K3), (3, 8, c(3, 2), K3a)):
-        x = V("land3", 3 * W, 3 * W + 16) if r == d else V("p3", 16 * d - 32, 16 * d - 16)
-        pick(x, qc(0, 128), hlist(i, a, k))
-        if r != d:
-            both("r3", [(d, land("land3", 0, d, 0, 6), V(x[0], x[1], x[1] + 6))])
-    if r >= 2:
-        B3 = one("B3")
-        lin(B3, V("pc", r, r + 1), 1.0, H2)
-    layers(3, B3, "or1" if r < 2 else "ord6")
-    fold(3)
-    olist(3, [c(3, 0)] if r == 1 else [])
-    count(4, picked(3))
-    refill(3)
-    lin(S3, c(3, 3), 1.0, V("pc", 3, 4))
-    lin(K4, S3, 0.25, K3)
-    lin(H3, S3, 1.0, H2)
-    scan(V("pb", 1, 3), cs(4, 2), V("zero", 0, 2), 0.0, A.add, A.add)
-    h = hlist(12, V("pb", 0, 3), K4, 3)
-    o = 3 * W - 16 * min(r, 2)
-    pick(V("cat4", o, o + 48), qc(0, 128), h)
-    far = topo.chip(C[N - 1]) != topo.chip(core)
-    n = 12 if far else 6
-    both("r4", [(d, land("cat4", 0, d, a, a + n), V("cat4", o + 16 * min(d, 2) + a, o + 16 * min(d, 2) + a + n))
-                for d, a in ((3, 0), (3, 6), (2, 0), (1, 0), (0, 0)) if d != r and not (far and a)])
+        plus(K7, Kb, c(2, far[0]), c(2, far[1]))
+    step(2, K7 if ex else K4)
+    kc = V("one", 42, 44)
+    lin(kc, V("c16", 0, 2), 1.0, Kb if x[1:] else K4)
+    if not x[1:]:
+        kc = plus(V("one", 40, 42), kc, c(2, r), c(2, near[0]))
+    calls(3, stage(3, 0, plus(oh(4, 2), kc, c(2, far[0]), c(2, far[1])), 0 if r < 2 else None), R3[r], [a] if join else [])
+    plus(K8, V(kc[0], kc[1], kc[1] + 1), c(2, far[0]), c(2, far[1]))
+    plus(K9, K8, c(3, 0))
+    a = part(3, stage(3, 32, plus(oh(6), K9, c(3, 1), c(3, 2)), 0 if ex else None), 3, 0, 6)
+    if not ex:
+        both([a])
+    if r == 2:
+        plus(K10, K9, c(3, 1))
+    K11 = plus(V("one", 44, 45), K9, c(3, 1), c(3, 2))
+    step(3, (K8, K8, K10, K11)[r])
+    plus(K12, K11, c(3, 3))
+    if 0 in far:
+        plus(oh(8), K11, c(3, 3))
+        plus(oh(9), K12, c(4, 0))
+    else:
+        plus(V("one", 45, 46), K11, c(4, 0))
+        plus(oh(8, 2), V("one", 44, 46), c(3, 3))
+    a = stage(4, 0, oh(8, 2), 16 * r if r < 2 else None)
+    b = stage(4, 32, plus(oh(10), K12, c(4, 0), c(4, 1)), 0 if r >= 2 else None)
+    p0, p1, p2 = part(4, a, 0, 0, 6), part(4, a, 1, 16, 6), part(4, b, 2, 0, 6)
+    p3 = [part(4, b, 3, 0, 12), part(4, b, 3, 0, 6), part(4, b, 3, 6, 6, 6)]
+    for x in (([p1, p2], p3[:1]), ([p0, p2] + p3[1:],), ([p1, p0], p3[:1]), ([p0, p1, p2],))[r]:
+        both(x)
+    if r:
+        plus(K13, K12, *[c(4, q) for q in range(min(r, 2))])
+    K = K13 if r else K12
     fold(4)
-    if r == 0:
-        B4 = H3
-    else:
-        lin(B4, V("pb", min(r, 2), min(r, 2) + 1), 1.0, H3)
-    if ex:
-        park(V("w4", 48, 128), qc(0, 80))
-        pick(V("w4", 0, 48), V("cat4", 0, 4 * W), order(4, B4, "or1", 3))
-        olist(4, [c(4, 2)])
-    else:
-        kq, ko, ka = [V("ki", i, i + 6) for i in (8, 16, 24)]
-        zk, zp, zm = [V("zk", i, i + 6) for i in (0, 8, 40)]
-        ts(kq, z0(4), 0.25, A.mult, -0.375, A.add)
-        ts(zk, kq, 1.0 / W, A.mult, float(N - 1 - r), A.add)
-        tt(zp, zk, z0(4), A.add)
-        ts(ko, zp, B4, A.add, float(W), A.mult)
-        ts(ka, ko, 4 * W - 1, A.bitwise_and)
-        tt(zm, ka, fv(4, M1, 6), A.max)
-        cp(V("of", 0, 6), zm)
-    for t, B in ((1, 0.0), (2, B2), (3, B3)):
-        signs(t)
-        numbers(t, B)
-        logpick(t)
-        renumber(t)
+    last = mlist(4, K)
+    olist(4)
+    log(4, K)
     lz = lambda a, w=1: V("lz", a, a + w)
-    lin(lz(1), own(1))
-    lin(lz(2), own(2), 1.0, lz(1))
-    lin(lz(3), own(3), 1.0, lz(2))
-    lin(lz(9), own(1), -1.0, 32.0)
-    lin(lz(10), own(2), -1.0, 32.0)
-    lin(lz(11), own(3), -1.0, 32.0)
+    iota(V("lzs", 0, 24), [[0, 6], [1, 4]], 0, 0, True)
+    act(V("lzk", 0, 24), V("lzs", 0, 24), F.Sign)
+    lin(V("lzt", 0, 24, 4), V("pw", 0, 6))
+    mine = V("b", L, 3 * 448, 448)
+    scan(lz(1, 3), mine, V("nul", 0, 3), 0.0, A.add, A.add)
+    lin(lz(9, 3), mine, -4.0, 32.0)
     for t in range(1, 4):
-        ts(lz(12 + 6 * t, 6), V("pw", 0, 6), lz(t), A.is_ge, lz(8 + t), A.mult)
-    tt(lz(12, 6), lz(18, 6), lz(24, 6), A.add)
-    tt(lz(36, 6), lz(30, 6), V("pw", 0, 6), A.add)
-    tt(lz(42, 6), lz(12, 6), lz(36, 6), A.add)
-    ts(V("lgl", 0, 6), lz(42, 6), 127.0, A.min)
-    signs(4)
-    logpick(4)
-    pick(V("lgo", 0, 96), V("lg", 0, 128), V("lgl", 0, 6))
-    gather(V("sidb", 0, 96), V("nl", 0, 128), V("lgl", 0, 6))
+        ts(V("lzt", t, 24, 4), V("pwq", 0, 6), lz(t), A.is_ge, lz(8 + t), A.mult)
+    scan(V("lzs", 0, 24), V("lzk", 0, 24), V("lzt", 0, 24), 0.0, A.mult, A.add)
+    ts(V("lgl", 0, 6), V("lzs", 3, 24, 4), 127.0, A.min)
+    pick(V("fin", 0, L), V("lg", 0, 128), V("lgl", 0, 6))
+    gather(V("sidb", 0, L), V("nl", 0, 128), V("lgl", 0, 6), 4.0)
 
-    def store(q, colo, src, n):
-        dma(q, T.oc[:, 4 * colo:4 * colo + 4 * n], code(src), [src], [])
-
-    def store_s(qs, colo, src, n):
-        s = pl(src)
+    def store(a, b):
+        src = V("fin", a, b)
+        dma("sy", T.oc[:, 4 * a:4 * b], code(src), [src], [], 8, 4 * (b - a))
         for k in range(4):
-            dma(qs[k], T.osc[4 * k:4 * k + 4, colo:colo + n], T[s[0]][32 * k:32 * k + 4, s[1]:s[1] + n], [s], [])
-    store("y", 0, V("lgo", 0, 96), 96)
-    store_s("yyyy", 0, V("lgo", 0, 96), 96)
-    dma("y", T.sid[:, 0:96], T.sidb[0:1, 0:96], [V("sidb", 0, 96)], [])
-    numbers(4, B4)
-    if not ex:
-        olist(4)
-    gather(V("sidb", 96, 192), V("num4", 0, 384), V("o4", 0, 6))
-    dma("y", T.sid[:, 96:192], T.sidb[0:1, 96:192], [V("sidb", 96, 192)], [])
+            dma("sy", T.osc[4 * k:4 * k + 4, a:b], T.fin_s[32 * k:32 * k + 4, a:b], [pl(src)], [], 1, b - a)
+        dma("sy", T.sid[:, a:b], T.sidb[0:1, a:b], [V("sidb", a, b)], [], 1, 4 * (b - a))
+    if not ONE[r]:
+        store(0, L)
+    gather(V("sidb", L, 2 * L), V("num4", 0, NO(4) + L + 8), O(4), 4.0)
     quant(V("vq", 0, 128), V("vt", 0, 512))
-    fin = V("fin", 0, 128)
-    pick(V("fin", 0, L), V(C4, 0, 384), V("o4" if ex else "of", 0, 6))
-    y, p = V("y_sb", 0, L), V("psD", 512, 512 + L)
-    if ex:
-        mm(V("psD", 512, 640), V("vq", 0, 128), V("w4", 256, 384))
-        lin(V("yw", 256, 256 + L), p)
-        mm(V("psC", 512, 640), V("vq", 0, 128), V("w4", 0, 128))
-        lin(V("yw", 0, 48), V("psC", 512, 560))
-        fill(V("yw", 48, 256), 0.0)
-        win, o4 = V("yw", 0, 256 + L), V("o4", 0, 6)
-        rec({"v": ("op", lambda e: e.tensor_copy(ap(y), ap(win).indirect(ap(o4))), 0.2), "s": ("op", lambda e: e.activation(ap(y), ap(win).indirect(ap(o4)), F.Copy), 0.22)}, [win, o4], [y])
-    else:
-        mm(V("psD", 512, 640), V("vq", 0, 128), fin)
-        rec({"v": ("op", lambda e: e.tensor_copy(ap(y), ap(p)), 0.16), "s": ("op", lambda e: e.activation(ap(y), ap(p), F.Copy), 0.19)}, [p], [y])
-    store("y", 96, V("fin", 0, L), L)
-    store_s("sysy", 96, V("fin", 0, L), L)
-    dma("s", T.y[:], T.y_sb[:], [y], [])
+    pick(V("fin", L, 2 * L), V("land4", 0, 4 * W + L), last)
+    y = V("y_sb", 0, L)
+    mm(V("psD", 512, 640), V("vq", 0, 128), V("fin", L, L + 128))
+    lin(y, V("psD", 512, 512 + L))
+    store(0 if ONE[r] else L, 2 * L)
+    dma("sy", T.y[:], T.y_sb[:], [y], [], 8, 4 * L)
     return {"nodes": nodes, "arrivals": arrivals, "sent": sent[0]}
 
 
-def joint(progs, more):
-    n = sum([len(p["nodes"]) for p in progs])
-    cur, x = [0.0] * n, 1
-    best = sched(progs, more, cur)
-    for _ in range(TRIES):
-        c = list(cur)
-        for _ in range(40):
-            x = (x * 1103515245 + 12345) % 2147483648
-            c[(x >> 8) % n] += (x % 251) / 250 - 0.5
-        y = sched(progs, more, c)
-        if y[0] <= best[0]:
-            best, cur = y, c
-    return best[1]
-
-
-def sched(progs, more, bias):
+def graph(progs):
     base, nodes = [], []
     for p in progs:
         base.append(len(nodes))
         nodes += p["nodes"]
     n = len(nodes)
     own = [k for k, p in enumerate(progs) for _ in p["nodes"]]
-    nxt, left, rows, seq = [[] for _ in range(n)], [0] * n, {}, []
+    nxt, far, left = [[] for _ in range(n)], [[] for _ in range(n)], [0] * n
     for k, p in enumerate(progs):
         for i, x in enumerate(p["nodes"]):
-            for j in x[5]:
-                y = p["nodes"][j]
-                nxt[base[k] + j].append((base[k] + i, 0.0 if "t" in x[0] and "t" in y[0] else y[4] + SEM))
+            for j in sorted(x[5]):
+                nxt[base[k] + j].append((base[k] + i, 0 if "t" in x[0] and "t" in p["nodes"][j][0] else 1))
                 left[base[k] + i] += 1
-            for d, key, lat, e in x[6]:
+            for d, key, es, size in x[6]:
                 j = base[d] + progs[d]["arrivals"][key]
-                nxt[base[k] + i].append((j, lat))
-                rows[(base[k] + i, j)] = max(rows.get((base[k] + i, j), 0), 128 // e)
+                far[base[k] + i].append((j, es, size))
                 left[j] += 1
     todo, lf, order = [i for i in range(n) if left[i] == 0], list(left), []
     while todo:
         i = todo.pop()
         order.append(i)
-        for j, _ in nxt[i]:
+        for j in [x[0] for x in nxt[i] + far[i]]:
             lf[j] -= 1
             if lf[j] == 0:
                 todo.append(j)
+    sem, fly, row, rate, _, _, _, lfly, lrow, _ = CASES[0]
     way = [0.0] * n
     for i in reversed(order):
-        way[i] = nodes[i][3] + max([w + way[j] for j, w in nxt[i]] + [nodes[i][4]])
-    way = [a + b for a, b in zip(way, bias)]
-    ready, free, avail = [0.0] * n, {}, [i for i in range(n) if left[i] == 0]
-    out = [[] for _ in progs]
+        late = lfly + nodes[i][4][0] * (lrow + nodes[i][4][1] / rate / 2) if nodes[i][4] else 0.0
+        way[i] = nodes[i][3] + max([late + s * sem + way[j] for j, s in nxt[i]] + [fly + 128 // len(es) * (row + size / rate) + way[j] for j, es, size in far[i]] + [late])
+    for i in range(n):
+        if nodes[i][4] and left[i] == 0:
+            way[i] = 1e5 - 10 * i
+    return nodes, own, base, nxt, far, left, way
 
-    def finish(i, t):
-        for j, w in nxt[i]:
-            ready[j] = max(ready[j], t + w)
+
+def table(G, case):
+    nodes, own, _, nxt, far = G[:5]
+    sem, fly, row, rate, cf, call, first, lfly, lrow, share = case
+    out = []
+    for i, x in enumerate(nodes):
+        out.append(({q: f[2] * cf if f[0] == "op" else call if f[0] == "remote" else f[2] for q, f in x[0].items()},
+                    x[4][0] * (lrow + x[4][1] / rate / 2) if x[4] else None,
+                    [(j, es, 128 // len(es) * (row + size / rate)) for j, es, size in far[i]], [(j, s * sem) for j, s in nxt[i]], own[i]))
+    return out, first - call, fly, lfly, share
+
+
+def play(tab, seq, state=None, trace=None):
+    t, first, fly, lfly, _ = tab
+    ready, free, eng, last, by = state or ([0.0] * len(t), {}, [[0.0] * 16 for _ in range(4)], {}, {})
+    end = acc = 0.0
+    for i, q in seq:
+        cost, io, fr, nx, k = t[i]
+        x = s = ready[i]
+        held = 0
+        if q:
+            kq = (k, q)
+            f = free.get(kq, 0.0)
+            if f > x:
+                x = s = f
+                held = 1
+            x += cost[q]
+            if fr:
+                if k not in free:
+                    free[k] = 1
+                    x += first
+                acc += x
+            free[kq] = x
+        if trace is not None:
+            why = (last.get(kq), 1) if held else (by.get(i), 0)
+            if q:
+                last[kq] = i
+        if io is not None:
+            e = eng[k]
+            x = max(x, max(e)) + io
+            e[:] = [x] * 16
+            x += lfly
+        for j, es, d in fr:
+            e = eng[k]
+            m = max(x, e[es[0]], e[es[-1]]) + d
+            for a in es:
+                e[a] = m
+            if m + fly > ready[j]:
+                ready[j] = m + fly
+                by[j] = i
+        for j, d in nx:
+            if x + d > ready[j]:
+                ready[j] = x + d
+                by[j] = i
+        if x > end:
+            end = x
+        if trace is not None:
+            trace[i] = (s, x, why)
+    return end, acc
+
+
+def worth(tabs, seq):
+    return sum([tab[4] * (lambda y: y[0] + EPS * y[1] / 80)(play(tab, seq)) for tab in tabs])
+
+
+def sched(G, tab, bias, qs):
+    nodes, own, base, nxt, far, left, way = G
+    n, left = len(nodes), list(left)
+    way = [a + b for a, b in zip(way, bias)]
+    state = ([0.0] * n, {}, [[0.0] * 16 for _ in base], {}, {})
+    ready, free = state[:2]
+    avail = {(k, q): [] for k in range(len(base)) for q in "vstgy"}
+    seq = []
+
+    def go(i, q):
+        seq.append((i, q))
+        play(tab, [(i, q)], state)
+        for j in [x[0] for x in nxt[i] + far[i]]:
             left[j] -= 1
             if left[j] == 0:
-                avail.append(j)
-    while avail:
+                new(j)
+
+    def new(i):
+        for q in qs[i]:
+            avail[(own[i], q)].append(i)
+        if not qs[i]:
+            go(i, None)
+    for i in [i for i in range(n) if left[i] == 0]:
+        new(i)
+    while True:
         best = None
-        for i in avail:
-            if not nodes[i][0]:
-                best = (0.0, i, None)
-                break
-            for q in nodes[i][0]:
-                s = max(free.get((own[i], q), 0.0), ready[i])
+        for kq, mine in avail.items():
+            if mine:
+                s = max(free.get(kq, 0.0), min([ready[j] for j in mine]))
                 if best is None or s < best[0]:
-                    best = (s, i, q)
-        s, i, q = best
-        if q is None:
-            avail.remove(i)
-            seq.append((i, None))
-            finish(i, ready[i])
-            continue
-        k = own[i]
-        f = free.get((k, q), 0.0)
-        mine = [j for j in avail if own[j] == k and q in nodes[j][0]]
-        i = max([j for j in mine if max(f, ready[j]) <= s], key=lambda j: (way[j], -j))
-        end = s + nodes[i][0][q][2]
-        soon = [j for j in mine if ready[j] < end - 0.02 and way[j] > way[i] + more]
+                    best = (s, kq)
+        if best is None:
+            return seq
+        s, (k, q) = best
+        mine = avail[(k, q)]
+        i = max([j for j in mine if ready[j] <= s], key=lambda j: (way[j], -j))
+        soon = [j for j in mine if ready[j] < s + nodes[i][0][q][2] - 0.02 and way[j] > way[i] + MORE]
         if soon:
             i = max(soon, key=lambda j: (way[j], -j))
-        avail.remove(i)
-        free[(k, q)] = max(f, ready[i]) + nodes[i][0][q][2]
-        out[k].append((q, i - base[k]))
-        seq.append((i, q))
-        finish(i, free[(k, q)])
-    total = 0.0
-    for dsem, dfly, drow, cf, call, share in CASES:
-        rdy, fr, end = [0.0] * n, {}, 0.0
-        for i, q in seq:
-            t = rdy[i]
-            if q is not None:
-                f = nodes[i][0][q]
-                t = max(t, fr.get((own[i], q), 0.0)) + f[2] * {"op": cf, "remote": call, "dma": 1.0}[f[0]]
-                fr[(own[i], q)] = t
-            end = max(end, t + nodes[i][4])
-            for j, w in nxt[i]:
-                w += dfly + drow * rows[(i, j)] if (i, j) in rows else dsem if w else 0.0
-                rdy[j] = max(rdy[j], t + w)
-        total += share * end
-    return total, out
+        for x in qs[i]:
+            avail[(k, x)].remove(i)
+        go(i, q)
+
+
+def joint(progs):
+    G = graph(progs)
+    nodes, own, base, nxt, far, left = G[:6]
+    n = len(nodes)
+    tabs = [table(G, c) for c in CASES]
+    seed = [1]
+
+    def rnd(k):
+        seed[0] = (seed[0] * 1103515245 + 12345) % 2147483648
+        return (seed[0] >> 8) % k
+    two = [i for i in range(n) if len(nodes[i][0]) > 1]
+    cur = ([0.0] * n, [list(y[0]) for y in nodes])
+    best = None
+    for it in range(TRIES):
+        c, qs = list(cur[0]), list(cur[1])
+        for _ in range(STEP[0] if it else 0):
+            c[rnd(n)] += rnd(251) / 250 - 0.5
+        for _ in range(STEP[1] if it else 0):
+            i = two[rnd(len(two))]
+            y = list(nodes[i][0])
+            qs[i] = ([y] + [[q] for q in y])[rnd(len(y) + 1)]
+        seq = sched(G, tabs[0], c, qs)
+        y = worth(tabs, seq)
+        if best is None or y <= best[0]:
+            best, cur = (y, seq), (c, qs)
+    suc = [set([x[0] for x in nxt[i] + far[i]]) for i in range(n)]
+    pre = [set() for _ in range(n)]
+    for i in range(n):
+        for j in suc[i]:
+            pre[j].add(i)
+    loads = set([i for i in range(n) if nodes[i][4] and left[i] == 0])
+    cur, pairs = best, None
+    for it in range(MOVES):
+        seq = cur[1]
+        if pairs is None:
+            pos, rows, pairs = {}, {}, []
+            for p, (i, q) in enumerate(seq):
+                pos[i] = p
+                rows.setdefault((own[i], q), []).append(i)
+            tr = {}
+            play(tabs[rnd(len(tabs))], seq, None, tr)
+            for v in [max(tr, key=lambda i: tr[i][1])] + [seq[n // 4 + rnd(n - n // 4)][0] for _ in range(3)]:
+                while v is not None:
+                    u, held = tr[v][2]
+                    if held and u not in loads:
+                        pairs.append((u, v))
+                    v = u
+        i, j = pairs[rnd(len(pairs))]
+        row, z = rows[(own[i], seq[pos[i]][1])], rnd(10)
+        if it % 40 == 0:
+            pairs = None
+        if z < 6:
+            if z < 3:
+                i = row[max(0, row.index(i) - (0, 0, 1, 2, 3)[rnd(5)])]
+                part, step, head, tail = suc, -1, j, i
+            else:
+                j = row[min(len(row) - 1, row.index(j) + (0, 0, 1, 2, 4, 8)[rnd(6)])]
+                part, step, head, tail = pre, 1, i, j
+            mid = seq[pos[i]:pos[j] + 1]
+            need = set([head])
+            for x, _ in mid[::step]:
+                if part[x] & need:
+                    need.add(x)
+            if tail in need or i in loads:
+                continue
+            new = seq[:pos[i]] + [x for x in mid if (x[0] in need) == (step < 0)] + [x for x in mid if (x[0] in need) != (step < 0)] + seq[pos[j] + 1:]
+        else:
+            x = (i, j, two[rnd(len(two))])[rnd(3)]
+            o = [q for q in nodes[x][0] if q != seq[pos[x]][1]]
+            if not o:
+                continue
+            new = list(seq)
+            new[pos[x]] = (x, o[rnd(len(o))])
+        y = worth(tabs, new)
+        if y <= cur[0] or rnd(1000) / 1000 < math.exp((cur[0] - y) / (HEAT * (1 - it / MOVES))):
+            if it % 8 == 0:
+                tr = {}
+                play(tabs[0], new, None, tr)
+                new = [x for _, _, x in sorted([(-1 if x[0] in loads else round(tr[x[0]][0], 6), p, x) for p, x in enumerate(new)])]
+                y = worth(tabs, new)
+            cur, pairs = (y, new), None
+            if y < best[0]:
+                best = cur
+    return best[1], G
 
 
 def rank_program(g, core, T, topo):
     r = T.rank_of(core)
     if r is None:
         return
-    progs = [program(q, T, topo) for q in range(len(T.cores))]
     if not PLAN:
-        PLAN.append(joint(progs, MORE))
+        PLAN.append(joint([program(q, T, topo) for q in range(len(T.cores))]))
+    progs = [program(q, T, topo) for q in range(len(T.cores))]
+    seq, G = PLAN[0]
     nodes, arrivals = progs[r]["nodes"], progs[r]["arrivals"]
     unit = {}
     for p in progs:
         for x in p["nodes"]:
-            for d, key, _, n in x[6]:
+            for d, key, es, _ in x[6]:
                 if d == r:
-                    unit[key] = unit.get(key, 0) + n
+                    unit[key] = unit.get(key, 0) + len(es)
     eng = {"v": g.vector, "s": g.scalar, "t": g.tensor, "g": g, "y": g.sync}
     done = {"v": 0, "s": 0, "t": 0, "g": 0}
     known = {q: {} for q in eng}
@@ -704,8 +856,10 @@ def rank_program(g, core, T, topo):
 
     for key, i in arrivals.items():
         note([], nodes[i][2], key, 1)
-    for q, i in PLAN[0][r]:
-        fns, reads, writes = nodes[i][:3]
+    for i, q in seq:
+        if G[1][i] != r or not q:
+            continue
+        fns, reads, writes = nodes[i - G[2][r]][:3]
         kind, fn, _ = fns[q]
         if kind == "op":
             key = "e" + q
@@ -715,7 +869,7 @@ def rank_program(g, core, T, topo):
             snap[(key, done[q])] = dict(known[q])
             note(reads, writes, key, done[q])
         elif kind == "dma":
-            key = "d%d" % ndma[0]
+            key = "e%d" % ndma[0]
             ndma[0] += 1
             unit[key] = 16
             deps(q, reads, writes, key)
@@ -726,8 +880,8 @@ def rank_program(g, core, T, topo):
             deps(q, reads, [], "remote")
             fn(eng[q])
     for k in range(ndma[0]):
-        if waited.get("d%d" % k, 0) < 1:
-            g.sync.wait_ge(T.sem["d%d" % k], 16)
+        if waited.get("e%d" % k, 0) < 1:
+            g.sync.wait_ge(T.sem["e%d" % k], 16)
     for q in "vstg":
         g.wait_ge(T.sem["e" + q], done[q])
     for k in arrivals:

import math
from concourse.bass import DstId, RemoteDMATransfer
from concourse.mybir import dt, AluOpType, ActivationFunctionType

A = AluOpType
F = ActivationFunctionType
f8, u8, f32, bf, i32, u16 = "float8_e4m3fn_x4", "uint8", "float32", "bfloat16", "int32", "uint16"
L = 96
W = 64
MODE = ["LRMM", "LLLM", "LLFM", "LMMM"]
R1 = [("1c0+12 2c0+12", "1s0+12", "3c0+24", "3s0+24 2c12+6 2s0+24"), ("0c0+30 3c0+30", "0s0+30 3s0+30", "2c0+18", "2s0+18"),
      ("1c0+12 0s0+48", "1s0+12", "3c0+24 0c0+24", "3s0+24 0c24+6"), ("0c0+30", "0s0+30", "2c0+18", "2s0+18 1s0+18", "1c0+12")]
R2 = [("1c0+12 2c0+12", "1s0+24 2c12+6 2s0+24"), ("2c0+18", "2s0+18"), ("1c0+12", "1s0+12"), ("2c0+18 1c0+18", "2s0+18 1s0+18")]
R3 = [("1c0+18", "1s0+18"), ("0c0+6", "0s0+6"), ("1c0+18 0c0+18", "1s0+18 0s0+18"), ("0c0+18 1c0+18", "0s0+18 1s0+18")]
LOADS = "q u x 0 1 2 3 Q v"
ONE = (0, 0, 0, 1)
TRIES, MOVES, HEAT, EPS = 250, 14000, 0.02, 1.0
STEP = (20, 6)
MORE = 0.6
CASES = [(0.11, 1.0, 0.02, 20e3, 1.0, 0.35, 1.4, 0.7, 0.015, 1.0), (0.11, 1.3, 0.012, 25e3, 0.8, 0.35, 1.2, 0.6, 0.008, 1.0),
         (0.15, 1.2, 0.04, 15e3, 1.0, 0.5, 1.8, 1.2, 0.02, 0.3)]
PLAN = []
SCRATCH, CODES = {}, []
for _w, _d, _ns in ((512, bf, "xt qt vt q1"), (2048, bf, "wt"), (768, bf, "jk"), (1024, bf, "h"),
                    (96, f32, "y_sb"), (192, f32, "sidb"), (128, f32, "nl j16 g384 gq nul"),
                    (16, i32, "pi qi"), (64, f32, "one lz posq"), (16, f32, "c16 pw pwq kh or1 pc pwm"), (4, f32, "kb ka"),
                    (32, bf, "cl1 cl2 cl3 cl4"), (112, bf, "sel cap"), (1792, bf, "b"), (24, f32, "lzt lzk lzs"),
                    (80, i32, "oi oj mi mj"), (8, u16, "lgl"), (16, u16, "oh ou"), (128, f32, "f1 f2 f3 f4"),
                    (64, u16, "o1 o2 o3 o4"), (384, f32, "num1 num2 num3 num4 hc1 hc2 hc3")):
    for _n in _ns.split():
        SCRATCH[_n] = ("sbuf", [128, _w], _d)
for _w, _ns in ((128, "xq qc vq lg d2 d3"), (256, "uq fin"), (512, "wq land1"), (272, "sr1 sr2 sr3 sf"),
                (384, "cat1 cat2 cat3 land2 land3 land4"), (64, "p2 p3 p4")):
    for _n in _ns.split():
        SCRATCH[_n] = ("sbuf", [128, _w], f8)
        SCRATCH[_n + "_s"] = ("sbuf", [128, _w], u8)
        CODES.append(_n)
for _n in ("psA", "psB", "psC", "psD"):
    SCRATCH[_n] = ("psum", [128, 1024], f32)
SEMAPHORES = ["ev", "es", "et", "eg", "loc", "r1", "r2", "r3", "r4"] + ["m%d%d" % (t, q) for t in range(1, 5) for q in range(4)] + ["e%d" % i for i in range(40)]


def fan(topo, src, dsts):
    off = [i for i, d in enumerate(dsts) if topo.chip(d) != topo.chip(src)]
    on = [i for i, d in enumerate(dsts) if topo.chip(d) == topo.chip(src)]
    out = [None] * len(dsts)
    used = []
    for part in (off, on):
        if not part:
            continue
        pool = [e for e in topo.engines(src, dsts[part[0]]) if e not in used]
        if part is on and not used:
            pool = pool[len(pool) // 2:]
        k = 1
        while 2 * k * len(part) <= len(pool):
            k *= 2
        for j, i in enumerate(part):
            out[i] = pool[j * k:(j + 1) * k]
        used += pool
    return out


def span(v):
    n, lo, hi = v[0], v[1], v[2]
    if n[:2] == "ps":
        return n, lo // 512 * 512, (hi + 511) // 512 * 512, None
    return n, lo, hi, (v[3], lo % v[3]) if v[3] > 1 else None


def meet(e, lo, hi, f):
    if e[0] >= hi or e[1] <= lo:
        return False
    for (s, a), p, q in ((e[5] or (1, 0), lo, hi), (f or (1, 0), e[0], e[1])):
        if (a - p) % s >= q - p:
            return False
    return e[5] is None or f is None or (e[5][1] - f[1]) % min(e[5][0], f[0]) == 0


def inside(e, lo, hi, f):
    return e[0] >= lo and e[1] <= hi and (f is None or e[5] == f)


def program(r, T, topo):
    C = T.cores
    N = len(C)
    core = C[r]
    others = [q for q in range(N) if q != r]
    near = [q for q in others if topo.chip(C[q]) == topo.chip(core)]
    far = [q for q in others if q not in near]
    ex = r == N - 1
    mode = " " + MODE[r]

    def RUN(t):
        return ((128, 0, 32, 32), (48, 48, 80, 32), (80, 80, 32, 32), (96, 32, 32, 48))[r][t - 1]

    def SW(t):
        return ("land%d" % t, 4 * W) if mode[t] == "M" else ("sf" if mode[t] == "F" else "sr%d" % t, RUN(t))

    def NO(t):
        return 256 if mode[t] == "R" else RUN(t)

    def NB(t):
        return t - 1 if mode[t] == "R" else t
    nodes, seen, arrivals = [], {}, {}
    sent, turn = [0], [0]

    def rec(fns, reads, writes, io=None, dests=()):
        i = len(nodes)
        pre = set()
        for isw, vs in ((0, reads), (1, writes)):
            for v in vs:
                n, lo, hi, f = span(v)
                pre.update([e[4] for e in seen.get(n, []) if meet(e, lo, hi, f) and (e[2] or isw or n[:2] == "ps")])
        for isw, vs in ((0, reads), (1, writes)):
            for v in vs:
                n, lo, hi, f = span(v)
                h = seen.setdefault(n, [])
                if isw:
                    h[:] = [e for e in h if not inside(e, lo, hi, f)]
                h.append((lo, hi, isw, "", i, f))
        nodes.append((fns, reads, writes, min([f[2] for f in fns.values()]) if fns else 0.0, io, pre, dests))

    def op(q, fn, reads, writes, cost):
        rec({q: ("op", fn, cost)}, reads, writes)

    def dma(qs, out, in_, reads, writes, rows, size):
        rec({q: ("dma", lambda e: e.dma_start(out, in_), 0.08) for q in qs}, reads, writes, (rows, size))

    def arrive(key, writes):
        arrivals[key] = len(nodes)
        rec({}, [], writes)

    def V(n, lo, hi, st=1):
        return (n, lo, hi, st)

    def ap(v):
        return T[v[0]][:, v[1]:v[2]] if v[3] == 1 else T[v[0]][:, v[1]:v[2]:v[3]]

    def code(v):
        return ap(v).bitcast(dt.uint8)

    def pl(v):
        return (v[0] + "_s",) + v[1:]

    def sc(x):
        return ap(x) if isinstance(x, tuple) else x

    def rd(*xs):
        return [x for x in xs if isinstance(x, tuple)]

    def w(v):
        return (v[2] - v[1] + v[3] - 1) // v[3]

    cols = {}

    def one(name):
        i = cols.setdefault(name, len(cols))
        return V("one", i, i + 1)

    def vcost(n):
        return 0.06 + 0.00105 * max(64, n)

    def tsf(out, in0, s1, op0, s2=None, op1=None):
        if op1 is None:
            return lambda e: e.tensor_scalar(ap(out), ap(in0), sc(s1), None, op0)
        return lambda e: e.tensor_scalar(ap(out), ap(in0), sc(s1), sc(s2), op0, op1)

    def ts(out, in0, s1, op0, s2=None, op1=None):
        op("v", tsf(out, in0, s1, op0, s2, op1), rd(in0, s1, s2), [out], vcost(w(out)))

    def tt(out, a, b, o):
        op("v", lambda e: e.tensor_tensor(ap(out), ap(a), ap(b), o), [a, b], [out], vcost(2 * w(out)))

    def cp(out, a):
        op("v", lambda e: e.tensor_copy(ap(out), ap(a)), [a], [out], vcost(w(out)))

    def actf(out, a, f, kw):
        k2 = {k: sc(x) for k, x in kw.items()}
        return lambda e: e.activation(ap(out), ap(a), f, **k2)

    def fill(out, c, qs="vg"):
        n = w(out) // (2 if SCRATCH[out[0]][2] == bf else 1)
        fns = {"v": ("op", lambda e: e.memset(ap(out), c), vcost(n)),
               "g": ("op", lambda e: e.iota(ap(out), [[0, w(out)]], int(c), 0, allow_small_or_imprecise_dtypes=True), 0.14 + 0.0018 * w(out)),
               "s": ("op", actf(out, V("nul", 0, w(out)), F.Identity, {"bias": c}), vcost(w(out)) + 0.03)}
        rec({q: fns[q] for q in qs}, [V("nul", 0, w(out))] if "s" in qs else [], [out])

    def scan(out, d0, d1, init, o0, o1):
        two = SCRATCH[out[0]][2] == bf
        op("v", lambda e: e.tensor_tensor_scan(ap(out), ap(d0), ap(d1), sc(init), o0, o1), rd(d0, d1, init), [out], vcost(w(out) // 2 if two else w(out)))

    def act(out, a, f, **kw):
        op("s", actf(out, a, f, kw), rd(a, kw.get("bias"), kw.get("scale")), [out] + rd(kw.get("accum_out")), vcost(w(out)) + 0.03)

    def lin(out, a, mul=1.0, add=0.0):
        x = 0.00105 * max(64, w(out))
        rec({"s": ("op", actf(out, a, F.Identity, {"scale": mul, "bias": add}), x + 0.09), "v": ("op", tsf(out, a, mul, A.mult, add, A.add), 0.06 + x)}, rd(a, mul, add), [out])

    def plus(out, a, *xs):
        if xs[1:] or SCRATCH[out[0]][2] == u16:
            ts(out, a, xs[0], A.add, *((xs[1], A.add) if xs[1:] else ()))
        else:
            lin(out, a, 1.0, xs[0])
        return out

    def relu(out, a):
        rec({"s": ("op", actf(out, a, F.Relu, {"scale": 0.0625}), vcost(w(out)) + 0.03), "v": ("op", tsf(out, a, 0.0, A.max, 0.0625, A.mult), vcost(w(out)))}, [a], [out])

    def quant(out, in_):
        op("v", lambda e: e.quantize_mx(ap(out), ap(pl(out)), ap(in_)), [in_], [out, pl(out)], 0.03 + 0.00025 * w(in_))

    def mm(out, l, x, start=True, stop=True):
        op("t", lambda e: e.matmul_mx(ap(out), ap(l), ap(pl(l)), ap(x), ap(pl(x)), start, stop), [l, pl(l), x, pl(x)], [out], 0.03 + 0.0011 * (w(x) + 16))

    def pick(out, win, off):
        op("v", lambda e: e.tensor_copy(ap(out).bitcast(dt.uint32), ap(win).bitcast(dt.uint32).indirect(ap(off))), [win, off], [out], 0.06 + 0.0014 * w(out))
        gather(pl(out), pl(win), off)

    def gather(out, win, off, mul=None):
        if mul:
            rec({"s": ("op", lambda e: e.activation(ap(out), ap(win).indirect(ap(off)), F.Identity, scale=mul), 0.08 + 0.0014 * w(out)),
                 "v": ("op", lambda e: e.tensor_scalar(ap(out), ap(win).indirect(ap(off)), mul, None, A.mult), 0.06 + 0.0014 * w(out))}, [win, off], [out])
        else:
            rec({"s": ("op", lambda e: e.activation(ap(out), ap(win).indirect(ap(off)), F.Copy), 0.08 + 0.0014 * w(out)),
                 "v": ("op", lambda e: e.tensor_copy(ap(out), ap(win).indirect(ap(off))), 0.06 + 0.0014 * w(out))}, [win, off], [out])

    def iota(out, pattern, base, cm, isf):
        kw = {"allow_small_or_imprecise_dtypes": True} if isf else {}
        op("g", lambda e: e.iota(ap(out), pattern, base, cm, **kw), [], [out], 0.14 + 0.0018 * w(out))

    def fused(moves, size=1):
        es = fan(topo, core, [C[m[0]] for m in moves])
        tr, reads, dests = [], [], []
        for (d, out, in_, sem), e in zip(moves, es):
            a = topo.addr(C[d])
            f, n = (code, 4 * w(in_)) if in_[0] in CODES else (ap, size * w(in_))
            tr.append(RemoteDMATransfer(dst_ids=[DstId(rid=a[0], pnc=a[1])], dma_engine_mask=sum(1 << k for k in e), remote_sem=T.sem[sem], src=f(in_), dst=f(out)))
            reads.append(in_)
            dests.append((d, sem, e, n))
            sent[0] += len(e)
        rec({"g": ("remote", lambda e: e.remote_dma_fused(tr, local_sem=T.sem.loc), 0.35)}, reads, [], None, dests)

    def scales(moves):
        return [(d, pl(a), pl(b), sem) for d, a, b, sem in moves]

    def both(moves):
        fused(moves)
        fused(scales(moves))

    def calls(t, x, cs, more=()):
        for i, call in enumerate(cs):
            moves = list((more, scales(more))[i]) if i < 2 else []
            for p in call.split():
                a, n = [int(y) for y in p[2:].split("+")]
                f = pl if p[1] == "s" else lambda v: v
                moves.append((int(p[0]), f(land(t, int(p[0]), a, n)), f(V(x[0], x[1] + a, x[1] + a + n)), "r%d" % t))
            fused(moves)

    def rot(t, d):
        return [q for q in range(N) if q != d and topo.chip(C[q]) == topo.chip(C[d])][0] if t == 1 else 0 if t == 2 and d < N - 1 else d

    def slot(t, m, d):
        return (2 * W if t == 1 else W) * ((m - rot(t, d) - 1) % N)

    def land(t, d, lo, n):
        return V("land%d" % t, slot(t, r, d) + lo, slot(t, r, d) + lo + n)

    def BV(t, o, lo, hi, st=1):
        return V("b", 448 * t - 448 + 112 * o + lo, 448 * t - 448 + 112 * o + hi, st)
    for t in range(1, 5):
        if mode[t] != "R":
            vs = [V("sf", 0, 32)] if mode[t] == "F" else [V("land%d" % t, slot(t, q, r), slot(t, q, r) + 48) for q in others]
            arrive("r%d" % t, vs + [pl(v) for v in vs])

    def c(t, q):
        return BV(t, 0, L, L + 1) if q == r else V("cl%d" % t, 8 * q, 8 * q + 1)
    for t in range(1, 5):
        for q in others:
            if t < 4 or q < 2 or (q == 2 and ex):
                arrive("m%d%d" % (t, q), [c(t, q)])

    loads = {"q": (V("q1", 0, 120), T.qx[:, 0:120]), "u": (V("xt", 120, 128), T.u[:, 0:8]), "x": (V("xt", 128, 512), T.x[:]),
             "Q": (V("qt", 0, 512), T.qx[:]), "v": (V("vt", 0, 512), T.v[:])}
    for i in range(4):
        loads[str(i)] = (V("wt", 512 * i, 512 * i + 512), T.w[:, 512 * i:512 * i + 512])
    for i, k in enumerate(LOADS.split()):
        dma("sy"[i % 2], ap(loads[k][0]), loads[k][1], [], [loads[k][0]], 8, 2 * w(loads[k][0]))
    lin(V("xt", 124, 128), V("xt", 124, 128), -1.0)

    iota(V("pi", 0, 16), [[0, 16]], 0, 1, False)
    iota(V("c16", 0, 16), [[16, 16]], 0, 0, True)
    iota(V("j16", 0, L), [[0, 6], [1, 16]], 0, 0, True)
    iota(V("g384", 0, 128), [[1, 128]], 384, 0, True)
    q16, pw, pwq = V("pw", 0, 1), V("pw", 0, 9), V("pwq", 0, 9)
    HS = 4 * max([RUN(t) for t in (1, 2, 3)])
    hs = V("h", HS, HS + 512)
    fill(V("h", HS + 4 * L, HS + 512), 0.0)
    if not r:
        fill(V("h", HS - 32, HS), 0.0)
    fill(V("nul", 0, 32), 0.0)
    fill(V("cap", 0, L), 6.0)
    fill(V("b", 0, 1792, 448), 0.0)
    fill(V("posq", 0, 64), 0.0)
    ts(V("ou", 0, 16), V("c16", 0, 16), 128.0, A.is_ge, 30.0, A.add)
    ts(V("qi", 0, 9), V("pi", 0, 9), 15, A.bitwise_and)
    tt(pw, V("qi", 0, 9), V("c16", 0, 9), A.add)
    lin(pwq, pw, 0.25)

    qc, xq = V("qc", 0, 128), V("xq", 0, 128)
    fill(V("q1", 120, 512), 0.0)
    fill(V("xt", 0, 120), 0.0)
    quant(land(1, r, 0, 128), V("q1", 0, 512))
    quant(xq, V("xt", 0, 512))
    calls(1, land(1, r, 0, 128), R1[r])
    for i in range(4):
        quant(V("wq", 128 * i, 128 * i + 128), V("wt", 512 * i, 512 * i + 512))
    for i in range(2):
        pick(V("uq", 128 * i, 128 * i + 128), V("xq", 0, 32), V("ou", 8 * i, 8 * i + 8))
    quant(qc, V("qt", 0, 512))
    for t in (1, 2, 3):
        if mode[t] in "LR":
            fill(V("o%d" % t, 6, 8), NO(t) + L, "v")
        else:
            quant(V("d%d" % t, 0, 128), V("xt", 0, 512))
    quant(V("fin", L, L + 128), V("xt", 0, 512))

    BANKS = [("psA", 0), ("psA", 512), ("psB", 0), ("psB", 512), ("psC", 0)]
    DB, PB, WB = ("psD", 0), ("psD", 512), ("psC", 512)

    def mult(src, h, n, at=0):
        for b in range(4):
            p, o = BANKS[turn[0] % 5]
            turn[0] += 1
            mm(V(p, o, o + w(src)), V("wq", 128 * b, 128 * b + 128), src)
            relu(V(h[0], h[1] + b, h[1] + 4 * n, 4), V(p, o + at, o + at + n))

    def diff(x, bank):
        d = V(bank[0], bank[1], bank[1] + w(x))
        mm(d, V("uq", 0, 128), x, True, False)
        mm(d, V("uq", 128, 256), x, False, True)
        return d

    def count(t, want):
        want(BV(t, 1, 0, L))
        scan(BV(t, 0, 1, L + 1), BV(t, 1, 0, L), V("cap", 0, L), 0.0, A.add, A.min)
        if t < 4 or not ex:
            fused([(d, V("cl%d" % t, 8 * r, 8 * r + 1), c(t, r), "m%d%d" % (t, r)) for d in (others if t < 4 or r < 2 else [N - 1])], 2)

    def straight(t, src, at=0):
        n, o = SW(t)
        s = V(n, o, o + 128)
        mult(src, hs, L, at)
        quant(s, hs)
        d = diff(s, DB)
        count(t, lambda out: ts(out, V(d[0], d[1], d[1] + L), 0.0, A.is_gt, 0.25, A.mult))

    straight(1, xq, 32)

    K0 = V("kh", 0, 1)
    lin(V("kh", 0, 2), V("pw", 0, 2), 1.0, (3 - r) / 4 - 0.375)
    ts(V("sel", 0, L), V("j16", 0, L), q16, A.is_equal, 512.0, A.mult)
    nq, ec, kn = one("nq"), one("ec"), one("kn")
    ts(V("pc", 0, 8), V("pw", 0, 8), (119.0, 71.0, 71.0, 95.0)[r], A.min)
    if r in (1, 2):
        lin(nq, q16, -1.0, 0.375 - 0.375 / (4 * W))
        lin(V("or1", 0, 5), V("pc", 0, 5), (W + 0.25) / (4 * W), nq)
        lin(V("or1", 8, 13), V("or1", 0, 5), 1.0, r / 4)
    lin(kn, K0, -1.0)
    lin(ec, q16, -4.0 * W, 1.5 * W - 0.375)
    lin(V("pwm", 0, 6), V("pw", 0, 6), 1.0, 4.0 * W)
    lin(V("gq", 0, 128), V("g384", 0, 128), 0.25, kn)
    lin(V("num1", NO(1), NO(1) + L), V("g384", 0, L), 0.25, (L * r - 384) / 4)
    lin(V("kb", 0, 2), V("pwq", 0, 2), 1.0, 0.125)
    pos = {}
    for t in range(1, 5):
        if NO(t) not in pos:
            a = 12 * len(pos)
            pos[NO(t)] = V("posq", a, a + 12)
            lin(V("posq", a + 1, a + 12, 2), V("pwq", 0, 6), 1.0, NO(t) / 4)
        fill(V("num%d" % NB(t), NO(t) + L, NO(t) + L + (32 if mode[t:t + 2] == "LR" else 8)), -0.25, "vs")

    def fv(t, lo, hi, st=1):
        return V("f%d" % t, lo, hi, st)
    z0 = lambda t: BV(t, 2, 15, L, 16)
    z1 = lambda t: BV(t, 3, 15, L, 16)
    na = lambda t: BV(t, 2, 7, L, 16)
    O = lambda t: V("o%d" % t, 0, 6)
    adds = lambda t: [c(t, q) for q in sorted(range(r), key=lambda q: q in far)][(0, 0, N if ex else 0, 0 if r < 2 else N, 0)[t]:] if t < 4 else [c(4, 2)] if ex else []

    def fold(t):
        scan(BV(t, 2, 0, L), V("sel", 0, L), BV(t, 0, 0, L), 0.0, A.add, A.min)
        scan(BV(t, 3, 0, L), V("sel", 0, L), BV(t, 0, 1, L + 1), 0.0, A.add, A.min)
        tt(na(t), z0(t), z1(t), A.is_equal)

    def olist(t):
        xs = adds(t)
        if mode[t] == "R":
            xs = [one("H")]
            lin(xs[0], K4, 1.0, kn)
        while xs:
            n = 2 - len(xs) % 2
            plus(z0(t), z0(t), *xs[:n])
            xs = xs[n:]
        scan(fv(t, 0, 12), pos[NO(t)], BV(t, 2, 7, L, 8), 0.0, A.mult, A.max)
        ts(O(t), fv(t, 1, 12, 2), 4.0, A.mult)

    def mlist(t, K):
        e = one("e%d" % t)
        lin(e, K, 4.0 * W, ec)
        for i, x in enumerate(adds(t)):
            e, y = one("e%d%d" % (t, i)), e
            lin(e, x, 4.0 * W + 1, y)
        tt(fv(t, 16, 22), na(t), V("pwm", 0, 6), A.mult)
        a, b = V("mi", 16 * t, 16 * t + 6), V("mj", 16 * t, 16 * t + 6)
        ts(a, z0(t), 4.0 * W + 1, A.mult, e, A.add)
        ts(b, a, 4 * W - 1, A.bitwise_and)
        tt(fv(t, 24, 30), b, fv(t, 16, 22), A.max)
        cp(V("o%d" % t, 32, 38), fv(t, 24, 30))
        return V("o%d" % t, 32, 38)

    def order(t, K):
        n = RUN(t) // 16
        a, x = (8 if rot(t, r) != r else 0), (2 * W if t == 1 else W)
        if t == 1:
            ts(V("oi", 16, 16 + n), V("pc", 0, n), x + 0.25, A.mult, x * (3 - rot(t, r)) - 0.375, A.add)
        else:
            ts(V("oi", 16 * t, 16 * t + n), V("or1", a, a + n), K, A.add, 4.0 * W, A.mult)
        ts(V("oj", 16 * t, 16 * t + n), V("oi", 16 * t, 16 * t + n), 4 * x - 1, A.bitwise_and)
        cp(V("o%d" % t, 16, 16 + n), V("oj", 16 * t, 16 * t + n))
        pick(V(SW(t)[0], 0, RUN(t)), V("land%d" % t, 0, 3 * x + ((30, 12, 18, 24)[r] if t < 3 else W)), V("o%d" % t, 16, 16 + n))

    def layer(t, at, n, wide):
        a = HS - 4 * (RUN(t) - at)
        to = NO(t) if mode[t] == "R" else at
        h, o = V("h", a, a + 512), V("cat%d" % NB(t), to, to + 128)
        mult(V("sr%d" % t, at, at + 128), h, n)
        quant(o, h)
        d = diff(o, PB if to else WB)
        lin(V("hc%d" % NB(t), to, to + wide), V(d[0], d[1], d[1] + wide))

    def log(t, K):
        for i in range(2):
            act(V("jk", L * (2 * t + i - 2), L * (2 * t + i - 1)), BV(t, 0, 1, L + 1), F.Sign, scale=-1.0, bias=V("kb", i, i + 1), accum_out=fv(t, 40 + i, 41 + i))
        n, o = SW(t)
        a = o // 32 * 32
        ls = V("o%d" % t, 8, 10)
        ts(ls, fv(t, 40, 42), 0.5, A.mult, 48.0 + o - a, A.add)
        pick(V("lg", 32 * t - 32, 32 * t), V(n, a, o + 128), ls)
        num = "num%d" % NB(t)
        if mode[t] != "R":
            lin(V(num, 0, NO(t)), V("gq", 0, NO(t)), 1.0, K)
        gather(V("nl", 32 * t - 32, 32 * t), V(num, NO(t) - o + a, NO(t) + L + 8), ls)
        if t < 4:
            gather(V("num%d" % NB(t + 1), NO(t + 1), NO(t + 1) + L), V(num, 0, NO(t) + L + 8), O(t))

    def step(t, K):
        n, o = SW(t)
        fold(t)
        if mode[t] in "LR":
            layer(t, o, L, 128 if mode[t:t + 2] == "LR" else L)
            if mode[t] == "L":
                order(t, K)
                if (r, t) == (1, 3):
                    ts(V("ka", 2, 4), V("pwq", 0, 2), 5.75, A.min, c(3, 0), A.add)
                    ts(V("oh", 12, 14), V("ka", 2, 4), c(3, 1), A.add, 4.0, A.mult)
                    pick(V("p4", 0, 32), V("sr3", 0, o), V("oh", 12, 14))
                    both([(2, V("sf", 0, 24), V("p4", 0, 24), "r3")])
                layer(t, 0, min(o, (120, 48, 80, 96)[r]), o)
            olist(t)
            o = NO(t)
            win = V("hc%d" % NB(t), 0, o + L)
            count(t + 1, lambda out: op("v", lambda e: e.tensor_scalar(ap(out), ap(win).indirect(ap(O(t))), 0.0, 0.25, A.is_gt, A.mult), [win, O(t)], [out], 0.06 + 0.0014 * L))
            m, a = SW(t + 1)
            pick(V(m, a, a + 128), V("cat%d" % NB(t), 0, o + 128), V("o%d" % t, 0, 8))
        else:
            if mode[t] == "F":
                olist(t)
            pick(V("d%d" % t, 0, L), V(n, 0, o + L), O(t) if mode[t] == "F" else mlist(t, K))
            straight(t + 1, V("d%d" % t, 0, 128))
            if mode[t] == "M":
                olist(t)
        log(t, K)

    def stage(t, at, ls, mine=None):
        x = V("p%d" % t, at, at + 16 * w(ls)) if mine is None else land(t, r, -mine, 16 * w(ls))
        pick(x, qc, ls)
        return x

    def part(t, x, d, a, n, lo=0):
        return (d, land(t, d, lo, n), V(x[0], x[1] + a, x[1] + a + n), "r%d" % t)
    oh = lambda i, n=1: V("oh", i, i + n)
    K4, K7, Kb, K8, K9, K10, K12, K13 = [one("K%d" % i) for i in range(8)]

    step(1, K0)
    ka = plus(V("ka", 0, 2), V("kh", 0, 2), c(1, r), c(1, near[0]))
    calls(2, stage(2, 0, plus(oh(0, 2), ka, c(1, far[0]), c(1, far[1])), 0 if r in (1, 2) else None), R2[r])
    plus(K4, V("ka", 0, 1), c(1, far[0]), c(1, far[1]))
    x = [q for q in [r] + near if q < N - 1]
    plus(Kb, K4, *[c(2, q) for q in x])
    a = part(2, stage(2, 32, plus(oh(2), Kb, *[c(2, q) for q in far if q < N - 1]), 0 if ex else None), 3, 0, 6)
    join = N - 1 in near
    if not ex and not join:
        both([a])
    if ex:
        plus(K7, Kb, c(2, far[0]), c(2, far[1]))
    step(2, K7 if ex else K4)
    kc = V("one", 42, 44)
    lin(kc, V("c16", 0, 2), 1.0, Kb if x[1:] else K4)
    if not x[1:]:
        kc = plus(V("one", 40, 42), kc, c(2, r), c(2, near[0]))
    calls(3, stage(3, 0, plus(oh(4, 2), kc, c(2, far[0]), c(2, far[1])), 0 if r < 2 else None), R3[r], [a] if join else [])
    plus(K8, V(kc[0], kc[1], kc[1] + 1), c(2, far[0]), c(2, far[1]))
    plus(K9, K8, c(3, 0))
    a = part(3, stage(3, 32, plus(oh(6), K9, c(3, 1), c(3, 2)), 0 if ex else None), 3, 0, 6)
    if not ex:
        both([a])
    if r == 2:
        plus(K10, K9, c(3, 1))
    K11 = plus(V("one", 44, 45), K9, c(3, 1), c(3, 2))
    step(3, (K8, K8, K10, K11)[r])
    plus(K12, K11, c(3, 3))
    if 0 in far:
        plus(oh(8), K11, c(3, 3))
        plus(oh(9), K12, c(4, 0))
    else:
        plus(V("one", 45, 46), K11, c(4, 0))
        plus(oh(8, 2), V("one", 44, 46), c(3, 3))
    a = stage(4, 0, oh(8, 2), 16 * r if r < 2 else None)
    b = stage(4, 32, plus(oh(10), K12, c(4, 0), c(4, 1)), 0 if r >= 2 else None)
    p0, p1, p2 = part(4, a, 0, 0, 6), part(4, a, 1, 16, 6), part(4, b, 2, 0, 6)
    p3 = [part(4, b, 3, 0, 12), part(4, b, 3, 0, 6), part(4, b, 3, 6, 6, 6)]
    for x in (([p1, p2], p3[:1]), ([p0, p2] + p3[1:],), ([p1, p0], p3[:1]), ([p0, p1, p2],))[r]:
        both(x)
    if r:
        plus(K13, K12, *[c(4, q) for q in range(min(r, 2))])
    K = K13 if r else K12
    fold(4)
    last = mlist(4, K)
    olist(4)
    log(4, K)
    lz = lambda a, w=1: V("lz", a, a + w)
    iota(V("lzs", 0, 24), [[0, 6], [1, 4]], 0, 0, True)
    act(V("lzk", 0, 24), V("lzs", 0, 24), F.Sign)
    lin(V("lzt", 0, 24, 4), V("pw", 0, 6))
    mine = V("b", L, 3 * 448, 448)
    scan(lz(1, 3), mine, V("nul", 0, 3), 0.0, A.add, A.add)
    lin(lz(9, 3), mine, -4.0, 32.0)
    for t in range(1, 4):
        ts(V("lzt", t, 24, 4), V("pwq", 0, 6), lz(t), A.is_ge, lz(8 + t), A.mult)
    scan(V("lzs", 0, 24), V("lzk", 0, 24), V("lzt", 0, 24), 0.0, A.mult, A.add)
    ts(V("lgl", 0, 6), V("lzs", 3, 24, 4), 127.0, A.min)
    pick(V("fin", 0, L), V("lg", 0, 128), V("lgl", 0, 6))
    gather(V("sidb", 0, L), V("nl", 0, 128), V("lgl", 0, 6), 4.0)

    def store(a, b):
        src = V("fin", a, b)
        dma("sy", T.oc[:, 4 * a:4 * b], code(src), [src], [], 8, 4 * (b - a))
        for k in range(4):
            dma("sy", T.osc[4 * k:4 * k + 4, a:b], T.fin_s[32 * k:32 * k + 4, a:b], [pl(src)], [], 1, b - a)
        dma("sy", T.sid[:, a:b], T.sidb[0:1, a:b], [V("sidb", a, b)], [], 1, 4 * (b - a))
    if not ONE[r]:
        store(0, L)
    gather(V("sidb", L, 2 * L), V("num4", 0, NO(4) + L + 8), O(4), 4.0)
    quant(V("vq", 0, 128), V("vt", 0, 512))
    pick(V("fin", L, 2 * L), V("land4", 0, 4 * W + L), last)
    y = V("y_sb", 0, L)
    mm(V("psD", 512, 640), V("vq", 0, 128), V("fin", L, L + 128))
    lin(y, V("psD", 512, 512 + L))
    store(0 if ONE[r] else L, 2 * L)
    dma("sy", T.y[:], T.y_sb[:], [y], [], 8, 4 * L)
    return {"nodes": nodes, "arrivals": arrivals, "sent": sent[0]}


def graph(progs):
    base, nodes = [], []
    for p in progs:
        base.append(len(nodes))
        nodes += p["nodes"]
    n = len(nodes)
    own = [k for k, p in enumerate(progs) for _ in p["nodes"]]
    nxt, far, left = [[] for _ in range(n)], [[] for _ in range(n)], [0] * n
    for k, p in enumerate(progs):
        for i, x in enumerate(p["nodes"]):
            for j in sorted(x[5]):
                nxt[base[k] + j].append((base[k] + i, 0 if "t" in x[0] and "t" in p["nodes"][j][0] else 1))
                left[base[k] + i] += 1
            for d, key, es, size in x[6]:
                j = base[d] + progs[d]["arrivals"][key]
                far[base[k] + i].append((j, es, size))
                left[j] += 1
    todo, lf, order = [i for i in range(n) if left[i] == 0], list(left), []
    while todo:
        i = todo.pop()
        order.append(i)
        for j in [x[0] for x in nxt[i] + far[i]]:
            lf[j] -= 1
            if lf[j] == 0:
                todo.append(j)
    sem, fly, row, rate, _, _, _, lfly, lrow, _ = CASES[0]
    way = [0.0] * n
    for i in reversed(order):
        late = lfly + nodes[i][4][0] * (lrow + nodes[i][4][1] / rate / 2) if nodes[i][4] else 0.0
        way[i] = nodes[i][3] + max([late + s * sem + way[j] for j, s in nxt[i]] + [fly + 128 // len(es) * (row + size / rate) + way[j] for j, es, size in far[i]] + [late])
    for i in range(n):
        if nodes[i][4] and left[i] == 0:
            way[i] = 1e5 - 10 * i
    return nodes, own, base, nxt, far, left, way


def table(G, case):
    nodes, own, _, nxt, far = G[:5]
    sem, fly, row, rate, cf, call, first, lfly, lrow, share = case
    out = []
    for i, x in enumerate(nodes):
        out.append(({q: f[2] * cf if f[0] == "op" else call if f[0] == "remote" else f[2] for q, f in x[0].items()},
                    x[4][0] * (lrow + x[4][1] / rate / 2) if x[4] else None,
                    [(j, es, 128 // len(es) * (row + size / rate)) for j, es, size in far[i]], [(j, s * sem) for j, s in nxt[i]], own[i]))
    return out, first - call, fly, lfly, share


def play(tab, seq, state=None, trace=None):
    t, first, fly, lfly, _ = tab
    ready, free, eng, last, by = state or ([0.0] * len(t), {}, [[0.0] * 16 for _ in range(4)], {}, {})
    end = acc = 0.0
    for i, q in seq:
        cost, io, fr, nx, k = t[i]
        x = s = ready[i]
        held = 0
        if q:
            kq = (k, q)
            f = free.get(kq, 0.0)
            if f > x:
                x = s = f
                held = 1
            x += cost[q]
            if fr:
                if k not in free:
                    free[k] = 1
                    x += first
                acc += x
            free[kq] = x
        if trace is not None:
            why = (last.get(kq), 1) if held else (by.get(i), 0)
            if q:
                last[kq] = i
        if io is not None:
            e = eng[k]
            x = max(x, max(e)) + io
            e[:] = [x] * 16
            x += lfly
        for j, es, d in fr:
            e = eng[k]
            m = max(x, e[es[0]], e[es[-1]]) + d
            for a in es:
                e[a] = m
            if m + fly > ready[j]:
                ready[j] = m + fly
                by[j] = i
        for j, d in nx:
            if x + d > ready[j]:
                ready[j] = x + d
                by[j] = i
        if x > end:
            end = x
        if trace is not None:
            trace[i] = (s, x, why)
    return end, acc


def worth(tabs, seq):
    return sum([tab[4] * (lambda y: y[0] + EPS * y[1] / 80)(play(tab, seq)) for tab in tabs])


def sched(G, tab, bias, qs):
    nodes, own, base, nxt, far, left, way = G
    n, left = len(nodes), list(left)
    way = [a + b for a, b in zip(way, bias)]
    state = ([0.0] * n, {}, [[0.0] * 16 for _ in base], {}, {})
    ready, free = state[:2]
    avail = {(k, q): [] for k in range(len(base)) for q in "vstgy"}
    seq = []

    def go(i, q):
        seq.append((i, q))
        play(tab, [(i, q)], state)
        for j in [x[0] for x in nxt[i] + far[i]]:
            left[j] -= 1
            if left[j] == 0:
                new(j)

    def new(i):
        for q in qs[i]:
            avail[(own[i], q)].append(i)
        if not qs[i]:
            go(i, None)
    for i in [i for i in range(n) if left[i] == 0]:
        new(i)
    while True:
        best = None
        for kq, mine in avail.items():
            if mine:
                s = max(free.get(kq, 0.0), min([ready[j] for j in mine]))
                if best is None or s < best[0]:
                    best = (s, kq)
        if best is None:
            return seq
        s, (k, q) = best
        mine = avail[(k, q)]
        i = max([j for j in mine if ready[j] <= s], key=lambda j: (way[j], -j))
        soon = [j for j in mine if ready[j] < s + nodes[i][0][q][2] - 0.02 and way[j] > way[i] + MORE]
        if soon:
            i = max(soon, key=lambda j: (way[j], -j))
        for x in qs[i]:
            avail[(k, x)].remove(i)
        go(i, q)


def joint(progs):
    G = graph(progs)
    nodes, own, base, nxt, far, left = G[:6]
    n = len(nodes)
    tabs = [table(G, c) for c in CASES]
    seed = [1]

    def rnd(k):
        seed[0] = (seed[0] * 1103515245 + 12345) % 2147483648
        return (seed[0] >> 8) % k
    two = [i for i in range(n) if len(nodes[i][0]) > 1]
    cur = ([0.0] * n, [list(y[0]) for y in nodes])
    best = None
    for it in range(TRIES):
        c, qs = list(cur[0]), list(cur[1])
        for _ in range(STEP[0] if it else 0):
            c[rnd(n)] += rnd(251) / 250 - 0.5
        for _ in range(STEP[1] if it else 0):
            i = two[rnd(len(two))]
            y = list(nodes[i][0])
            qs[i] = ([y] + [[q] for q in y])[rnd(len(y) + 1)]
        seq = sched(G, tabs[0], c, qs)
        y = worth(tabs, seq)
        if best is None or y <= best[0]:
            best, cur = (y, seq), (c, qs)
    suc = [set([x[0] for x in nxt[i] + far[i]]) for i in range(n)]
    pre = [set() for _ in range(n)]
    for i in range(n):
        for j in suc[i]:
            pre[j].add(i)
    loads = set([i for i in range(n) if nodes[i][4] and left[i] == 0])
    cur, pairs = best, None
    for it in range(MOVES):
        seq = cur[1]
        if pairs is None:
            pos, rows, pairs = {}, {}, []
            for p, (i, q) in enumerate(seq):
                pos[i] = p
                rows.setdefault((own[i], q), []).append(i)
            tr = {}
            play(tabs[rnd(len(tabs))], seq, None, tr)
            for v in [max(tr, key=lambda i: tr[i][1])] + [seq[n // 4 + rnd(n - n // 4)][0] for _ in range(3)]:
                while v is not None:
                    u, held = tr[v][2]
                    if held and u not in loads:
                        pairs.append((u, v))
                    v = u
        i, j = pairs[rnd(len(pairs))]
        row, z = rows[(own[i], seq[pos[i]][1])], rnd(10)
        if it % 40 == 0:
            pairs = None
        if z < 6:
            if z < 3:
                i = row[max(0, row.index(i) - (0, 0, 1, 2, 3)[rnd(5)])]
                part, step, head, tail = suc, -1, j, i
            else:
                j = row[min(len(row) - 1, row.index(j) + (0, 0, 1, 2, 4, 8)[rnd(6)])]
                part, step, head, tail = pre, 1, i, j
            mid = seq[pos[i]:pos[j] + 1]
            need = set([head])
            for x, _ in mid[::step]:
                if part[x] & need:
                    need.add(x)
            if tail in need or i in loads:
                continue
            new = seq[:pos[i]] + [x for x in mid if (x[0] in need) == (step < 0)] + [x for x in mid if (x[0] in need) != (step < 0)] + seq[pos[j] + 1:]
        else:
            x = (i, j, two[rnd(len(two))])[rnd(3)]
            o = [q for q in nodes[x][0] if q != seq[pos[x]][1]]
            if not o:
                continue
            new = list(seq)
            new[pos[x]] = (x, o[rnd(len(o))])
        y = worth(tabs, new)
        if y <= cur[0] or rnd(1000) / 1000 < math.exp((cur[0] - y) / (HEAT * (1 - it / MOVES))):
            if it % 8 == 0:
                tr = {}
                play(tabs[0], new, None, tr)
                new = [x for _, _, x in sorted([(-1 if x[0] in loads else round(tr[x[0]][0], 6), p, x) for p, x in enumerate(new)])]
                y = worth(tabs, new)
            cur, pairs = (y, new), None
            if y < best[0]:
                best = cur
    return best[1], G


def rank_program(g, core, T, topo):
    r = T.rank_of(core)
    if r is None:
        return
    if not PLAN:
        PLAN.append(joint([program(q, T, topo) for q in range(len(T.cores))]))
    progs = [program(q, T, topo) for q in range(len(T.cores))]
    seq, G = PLAN[0]
    nodes, arrivals = progs[r]["nodes"], progs[r]["arrivals"]
    unit = {}
    for p in progs:
        for x in p["nodes"]:
            for d, key, es, _ in x[6]:
                if d == r:
                    unit[key] = unit.get(key, 0) + len(es)
    eng = {"v": g.vector, "s": g.scalar, "t": g.tensor, "g": g, "y": g.sync}
    done = {"v": 0, "s": 0, "t": 0, "g": 0}
    known = {q: {} for q in eng}
    snap, hist, waited = {}, {}, {}
    ndma = [0]

    def deps(q, reads, writes, key):
        need = {}
        for isw, vs in ((0, reads), (1, writes)):
            for v in vs:
                n, lo, hi, f = span(v)
                for e in hist.get(n, []):
                    w, k, i = e[2:5]
                    if not meet(e, lo, hi, f) or (k == key == "et" and n[:2] == "ps"):
                        continue
                    if not (w or isw or (n[:2] == "ps" and k != key)):
                        continue
                    if need.get(k, 0) < i:
                        need[k] = i
        for k in sorted(need):
            i = need[k]
            if known[q].get(k, 0) >= i:
                continue
            eng[q].wait_ge(T.sem[k], i * unit.get(k, 1))
            waited[k] = max(waited.get(k, 0), i)
            for kk, ii in snap.get((k, i), {}).items():
                if known[q].get(kk, 0) < ii:
                    known[q][kk] = ii
            known[q][k] = max(known[q].get(k, 0), i)

    def note(reads, writes, key, idx):
        for isw, vs in ((0, reads), (1, writes)):
            for v in vs:
                n, lo, hi, f = span(v)
                h = hist.setdefault(n, [])
                h[:] = [e for e in h if not (inside(e, lo, hi, f) and (isw or (e[3] == key and not e[2])))]
                h.append((lo, hi, isw, key, idx, f))

    for key, i in arrivals.items():
        note([], nodes[i][2], key, 1)
    for i, q in seq:
        if G[1][i] != r or not q:
            continue
        fns, reads, writes = nodes[i - G[2][r]][:3]
        kind, fn, _ = fns[q]
        if kind == "op":
            key = "e" + q
            deps(q, reads, writes, key)
            done[q] += 1
            fn(eng[q]).then_inc(T.sem[key], 1)
            snap[(key, done[q])] = dict(known[q])
            note(reads, writes, key, done[q])
        elif kind == "dma":
            key = "e%d" % ndma[0]
            ndma[0] += 1
            unit[key] = 16
            deps(q, reads, writes, key)
            fn(eng[q]).then_inc(T.sem[key], 16)
            snap[(key, 1)] = dict(known[q])
            note(reads, writes, key, 1)
        else:
            deps(q, reads, [], "remote")
            fn(eng[q])
    for k in range(ndma[0]):
        if waited.get("e%d" % k, 0) < 1:
            g.sync.wait_ge(T.sem["e%d" % k], 16)
    for q in "vstg":
        g.wait_ge(T.sem["e" + q], done[q])
    for k in arrivals:
        g.wait_ge(T.sem[k], unit[k])
    g.wait_ge(T.sem.loc, progs[r]["sent"])
